import numpy as np
import ml_dtypes


def mxq(x, axis, fmt="e4m3"):
    dtype, down = {"e4m3": (ml_dtypes.float8_e4m3fn, 7), "e5m2": (ml_dtypes.float8_e5m2, 14)}[fmt]
    v = np.moveaxis(np.asarray(x, np.float32).astype(ml_dtypes.bfloat16).astype(np.float64), axis, -1)
    blocks = v.reshape(v.shape[:-1] + (-1, 32))
    amax = np.abs(blocks).max(-1, keepdims=True)
    byte = np.maximum(np.where(amax > 0, np.frexp(amax)[1] - 1 + 127, 0) - down, 1)
    scale = np.exp2(byte - 127.0)
    codes = (blocks / scale).astype(np.float32).astype(dtype).astype(np.float64)
    return np.moveaxis((codes * scale).reshape(v.shape), -1, axis)


WIDE = False


def mx_kscale(k):
    if not WIDE:
        return np.ones(k)
    levels = np.array([10, -10, 5, -5, 0])
    if k % 512:
        return np.exp2(np.random.permutation(np.resize(levels, k // 32))).repeat(32)
    a = np.empty((k // 512, 16))
    for p in range(k // 512):
        a[p, :8] = np.random.permutation(np.resize(levels, 8))
        for g in range(8):
            far = levels[np.abs(levels - a[p, g]) >= 10]
            a[p, g + 8] = far[np.random.randint(len(far))]
    return np.exp2(a.ravel()).repeat(32)


def f64(x):
    return np.asarray(x).astype(np.float64)


def striped(idx):
    return np.tile(idx.reshape(-1, 16).T, (8, 1)).astype(np.uint16)


def unstriped(offs):
    return offs[:16].T.reshape(-1).astype(np.int64)


E2M1 = np.array([0.0, 0.5, 1.0, 1.5, 2.0, 3.0, 4.0, 6.0, -0.0, -0.5, -1.0, -1.5, -2.0, -3.0, -4.0, -6.0])


def pack_weight(w, fmt):
    k, n = w.shape
    w = f64(np.asarray(w, np.float32).astype(ml_dtypes.bfloat16)).reshape(k // 32, 32, n)
    amax = np.abs(w).max(1)
    if fmt == "e4m3":
        byte = np.frexp(amax)[1] - 1 + 127 - 7
    else:
        mant, ex = np.frexp(amax / 6.0)
        byte = np.where(mant > 0.5, ex, ex - 1) + 127
    byte = np.clip(np.where(amax > 0, byte, 1), 1, 254)
    scaled = (w * np.exp2(127.0 - byte)[:, None, :]).reshape(k, n).astype(np.float32)
    by_word = np.ascontiguousarray(scaled.reshape(k // 512, 128, 4, n).transpose(0, 1, 3, 2))
    if fmt == "e4m3":
        words = by_word.astype(ml_dtypes.float8_e4m3fn).view(np.uint8)
    else:
        c = by_word.astype(ml_dtypes.float4_e2m1fn).view(np.uint8) & 0xF
        words = (c[..., 0::2] | (c[..., 1::2] << 4)).reshape(k // 512, 128, 2 * n)
    return np.ascontiguousarray(words), np.ascontiguousarray(byte.astype(np.uint8).reshape(k // 512, 16, n))


def unpack_weight(words, scales, fmt):
    g, _, n = scales.shape
    words = np.ascontiguousarray(words).reshape(g, 128, n, -1)
    if fmt == "e4m3":
        vals = words.view(ml_dtypes.float8_e4m3fn).astype(np.float64)
    else:
        nib = np.empty((g, 128, n, 4), np.uint8)
        nib[..., 0::2] = words & 0xF
        nib[..., 1::2] = words >> 4
        vals = E2M1[nib]
    vals = vals * np.repeat(np.exp2(scales.astype(np.float64) - 127.0), 8, axis=1)[..., None]
    return vals.transpose(0, 1, 3, 2).reshape(g * 512, n)


def sigmoid(v):
    return 1.0 / (1.0 + np.exp(-np.maximum(v, -700.0)))


K, T, E, H, N = 512, 1024, 2, 1024, 128
COUNTS = (640, 384)
STARTS = np.cumsum((0,) + COUNTS)


def by_expert(wq, xq):
    return np.concatenate([wq[e].T @ xq[:, STARTS[e]:STARTS[e + 1]] for e in range(E)], axis=1)


def setup_inputs():
    n = np.random.standard_normal
    s = mx_kscale(K)[:, None]
    u = mx_kscale(H)
    expert = np.random.permutation(np.repeat(np.arange(E), COUNTS))
    slot_token = np.argsort(expert, kind="stable")
    w1 = [pack_weight(m, "e2m1") for m in n((E, K, H)) / np.sqrt(K) / s[None]]
    w3 = [pack_weight(m, "e2m1") for m in n((E, K, H)) / np.sqrt(K) / s[None] * u[None, None, :]]
    w2 = [pack_weight(m, "e2m1") for m in n((E, H, N)) / np.sqrt(H) / u[None, :, None]]
    return {
        "xT": (n((K, T)) * s).astype(np.float32),
        "w1_words": np.stack([m[0] for m in w1]),
        "w1_scales": np.stack([m[1] for m in w1]),
        "w3_words": np.stack([m[0] for m in w3]),
        "w3_scales": np.stack([m[1] for m in w3]),
        "w2_words": np.stack([m[0] for m in w2]),
        "w2_scales": np.stack([m[1] for m in w2]),
        "gate": np.tile(np.random.uniform(0.2, 1.0, T), (N, 1)).astype(np.float32),
        "offs": striped(slot_token),
    }


def reference(xT, w1_words, w1_scales, w3_words, w3_scales, w2_words, w2_scales, gate, offs):
    idx = unstriped(offs)
    w1 = np.stack([unpack_weight(w1_words[e], w1_scales[e], "e2m1") for e in range(E)])
    w3 = np.stack([unpack_weight(w3_words[e], w3_scales[e], "e2m1") for e in range(E)])
    w2 = np.stack([unpack_weight(w2_words[e], w2_scales[e], "e2m1") for e in range(E)])
    xq = mxq(f64(xT)[:, idx], 0, "e4m3")
    h = sigmoid(by_expert(w1, xq))
    h = h * by_expert(w3, xq)
    y = by_expert(w2, mxq(h, 0, "e4m3"))
    out = np.zeros((N, T))
    out[:, idx] = f64(gate) * y
    return out

@@ -1,0 +1,202 @@
+from contextlib import ExitStack
+
+import concourse.mybir as mybir
+from concourse.masks import make_identity
+
+K, T, E, H, N = 512, 1024, 2, 1024, 128
+COUNTS = (640, 384)
+FLOPS = 2 * T * (2 * K * H + H * N)
+
+P = 128
+F32 = mybir.dt.float32
+BF16 = mybir.dt.bfloat16
+I32 = mybir.dt.int32
+U32 = mybir.dt.uint32
+U16 = mybir.dt.uint16
+U8 = mybir.dt.uint8
+FP8X4 = mybir.dt.float8_e4m3fn_x4
+FP4X4 = mybir.dt.float4_e2m1fn_x4
+MULT = mybir.AluOpType.mult
+SIGMOID = mybir.ActivationFunctionType.Sigmoid
+
+HALF = 512
+GROUPS = H // HALF
+BLOCKS = T // P
+X_CHUNKS = ((0, 512), (512, 768), (768, 1024))
+SCALAR_SHARE = 3
+GATHERS = ((0, 128), (128, 384), (384, 640), (640, 896), (896, 1024))
+SCATTERS = ((0, 2), (2, 4), (4, 5), (5, 7), (7, 8))
+
+
+def tile_moe_rag_glu_sigmoid_kernel(
+    tc, xT, w1_words, w1_scales, w3_words, w3_scales, w2_words, w2_scales, gate, offs, out
+):
+    nc = tc.nc
+    with ExitStack() as ctx:
+        keep = ctx.enter_context(tc.tile_pool(name="keep", bufs=1))
+        work = ctx.enter_context(tc.tile_pool(name="work", bufs=3))
+        psum_ab = ctx.enter_context(tc.psum_pool(name="psum_ab", bufs=3))
+        psum_ty = ctx.enter_context(tc.psum_pool(name="psum_ty", bufs=1))
+
+        x_bytes = keep.tile([P, T], U8, name="x_bytes", align_bytes=64)
+        nc.gpsimd.memset(x_bytes[:], 0)
+
+        def scale_plane(name, scales, passes, width, queue):
+            plane = keep.tile([P, passes, width], U8, name=name, align_bytes=64)
+            nc.vector.memset(plane[:].rearrange("p s i -> p (s i)").bitcast(I32), 0)
+            rows = scales.rearrange("e s (a r) i -> r a (e s) i", r=4)
+            for r in range(4):
+                queue.dma_start(out=plane[r:P:32].bitcast(I32), in_=rows[r].bitcast(I32))
+            return plane
+
+        identity = keep.tile([P, P], F32, name="identity")
+        make_identity(nc, identity[:])
+        warm = keep.tile([P, 1], F32, name="warm")
+        nc.vector.memset(warm[:], 0.0)
+        nc.scalar.activation(warm[:], warm[:], SIGMOID)
+
+        w1_plane = scale_plane("w1s", w1_scales, E, H, nc.scalar)
+        x_rows = xT.rearrange("(p j) w -> p j w", j=4)
+        x_raw = []
+        for c0, c1 in X_CHUNKS:
+            raw = keep.tile([P, 4, c1 - c0], F32, name="raw%d" % c0)
+            nc.sync.dma_start(out=raw[:], in_=x_rows[:, :, c0:c1])
+            x_raw.append(raw)
+        offsets = keep.tile([P, T // 16], U16, name="offsets")
+        nc.sync.dma_start(offsets[:], offs)
+        w3_plane = scale_plane("w3s", w3_scales, E, H, nc.sync)
+
+        w1_sb, w3_sb = [], []
+        gate_sb = keep.tile([P, T], F32, name="gate_sb")
+        w2_sb = keep.tile([P, E * GROUPS, 2 * N], U8, name="w2_sb", align_bytes=64)
+        for e in range(E):
+            for dst, src, name in ((w1_sb, w1_words, "w1_%d"), (w3_sb, w3_words, "w3_%d")):
+                words = keep.tile([P, 2 * H], U8, name=name % e, align_bytes=64)
+                nc.sync.dma_start(out=words[:].bitcast(I32), in_=src[e, 0].bitcast(I32))
+                dst.append(words)
+            if e == 0:
+                w2_plane = scale_plane("w2s", w2_scales, E * GROUPS, N, nc.sync)
+                nc.sync.dma_start(
+                    out=w2_sb[:].bitcast(I32), in_=w2_words.rearrange("e s p n -> p (e s) n").bitcast(I32)
+                )
+                nc.sync.dma_start(out=gate_sb[:], in_=gate)
+
+        x_words = keep.tile([P, T], U32, name="x_words", align_bytes=64)
+        for raw, (c0, c1) in zip(x_raw, X_CHUNKS):
+            width = c1 - c0
+            cut = width - width * SCALAR_SHARE // 8
+            side = keep.tile([P, width, 4], BF16, name="side%d" % c0, align_bytes=64)
+            view = raw[:].rearrange("p j w -> p w j")
+            nc.vector.tensor_copy(out=side[:, :cut, :], in_=view[:, :cut, :])
+            nc.scalar.copy(out=side[:, cut:, :], in_=view[:, cut:, :])
+            nc.vector.quantize_mx(
+                out=x_words[:, c0:c1].bitcast(FP8X4),
+                scales=x_bytes[:, c0:c1],
+                in_=side[:].rearrange("p w j -> p (w j)"),
+            )
+
+        slot_words, slot_bytes = {}, {}
+
+        def gather(g):
+            s0, s1 = GATHERS[g]
+            listed = offsets[:, s0 // 16 : s1 // 16]
+            words = keep.tile([P, s1 - s0], U32, name="slot_words%d" % g, align_bytes=64)
+            nc.vector.tensor_copy(words[:], x_words[:].indirect(listed))
+            scale = keep.tile([P, s1 - s0], U8, name="slot_bytes%d" % g, align_bytes=64)
+            nc.vector.tensor_copy(scale[:], x_bytes[:].indirect(listed))
+            for s in range(s0, s1, P):
+                slot_words[s // P] = words[:, s - s0 : s - s0 + P]
+                slot_bytes[s // P] = scale[:, s - s0 : s - s0 + P]
+
+        hidden, h_codes, h_bytes, y_banks = {}, {}, {}, {}
+
+        def first_layer(b):
+            e = 0 if b * P < COUNTS[0] else 1
+            h_rows = work.tile([P, GROUPS, HALF], BF16, name="h_rows", align_bytes=64)
+            for g in range(GROUPS):
+                banks = []
+                for words, plane, tag in ((w1_sb[e], w1_plane, "a"), (w3_sb[e], w3_plane, "b")):
+                    bank = psum_ab.tile([P, HALF], F32, name=tag)
+                    nc.tensor.matmul_mx(
+                        out=bank[:],
+                        lhsT=slot_words[b].bitcast(FP8X4),
+                        lhsT_scale=slot_bytes[b],
+                        rhs=words[:, 2 * HALF * g : 2 * HALF * (g + 1)].bitcast(FP4X4),
+                        rhs_scale=plane[:, e, HALF * g : HALF * (g + 1)],
+                        start=True,
+                        stop=True,
+                    )
+                    banks.append(bank[:].rearrange("s (p u d) -> s u p d", u=2, d=2))
+                gated = work.tile([P, HALF], F32, name="gated")
+                gated_view = gated[:].rearrange("s (u p d) -> s u p d", u=2, d=2)
+                nc.scalar.activation(gated_view, banks[0], SIGMOID)
+                nc.vector.tensor_tensor(
+                    h_rows[:, g, :].rearrange("s (u p d) -> s u p d", u=2, d=2), banks[1], gated_view, MULT
+                )
+            hidden[b] = h_rows
+
+        def turn(b):
+            words = hidden[b][:].rearrange("s g c -> s (g c)").bitcast(F32)
+            turned = psum_ty.tile([P, GROUPS, 2, P], F32, name="turned")
+            for g in range(GROUPS):
+                for u in range(2):
+                    at = (2 * g + u) * P
+                    nc.tensor.transpose(turned[:, g, u, :], words[:, at : at + P], identity[:])
+            quads = work.tile([P, GROUPS * P * 4], BF16, name="quads", align_bytes=64)
+            nc.scalar.copy(
+                out=quads[:].bitcast(F32).rearrange("p (g s u) -> p g s u", g=GROUPS, u=2),
+                in_=turned[:].rearrange("p g u s -> p g s u"),
+            )
+            codes = work.tile([P, GROUPS, P], U32, name="codes", align_bytes=64)
+            scale = work.tile([P, GROUPS, P], U8, name="scale", align_bytes=64)
+            nc.vector.quantize_mx(
+                out=codes[:].rearrange("p g s -> p (g s)").bitcast(FP8X4),
+                scales=scale[:].rearrange("p g s -> p (g s)"),
+                in_=quads[:],
+            )
+            h_codes[b], h_bytes[b] = codes, scale
+
+        outT = keep.tile([P, T], F32, name="outT")
+
+        def second_layer(b):
+            e = 0 if b * P < COUNTS[0] else 1
+            first, last = [s for s in SCATTERS if s[0] <= b < s[1]][0]
+            if b == first:
+                y_banks[first] = psum_ty.tile([P, 2 * P], F32, name="y")
+            y = y_banks[first]
+            for g in range(GROUPS):
+                nc.tensor.matmul_mx(
+                    out=y[:, (b - first) * P : (b - first + 1) * P],
+                    lhsT=w2_sb[:, e * GROUPS + g, :].bitcast(FP4X4),
+                    lhsT_scale=w2_plane[:, e * GROUPS + g, :],
+                    rhs=h_codes[b][:, g, :].bitcast(FP8X4),
+                    rhs_scale=h_bytes[b][:, g, :],
+                    start=(g == 0),
+                    stop=(g == GROUPS - 1),
+                )
+            if b == last - 1:
+                width = (last - first) * P
+                results = work.tile([P, width], F32, name="results%d" % width)
+                nc.scalar.copy(out=results[:], in_=y[:, :width])
+                listed = offsets[:, first * P // 16 : last * P // 16]
+                nc.vector.tensor_tensor(
+                    outT[:].indirect(listed), results[:], gate_sb[:, first * P : last * P], MULT
+                )
+
+        gather(0)
+        first_layer(0)
+        gather(1)
+        first_layer(1)
+        turn(0)
+        gather(2)
+        for b in range(2, BLOCKS + 2):
+            if b == 4:
+                gather(3)
+            if b == 6:
+                gather(4)
+            if b < BLOCKS:
+                first_layer(b)
+            if b - 1 < BLOCKS:
+                turn(b - 1)
+            second_layer(b - 2)
+        nc.sync.dma_start(out=out, in_=outT[:])

@@ -22,9 +22,9 @@ SIGMOID = mybir.ActivationFunctionType.Sigmoid
 HALF = 512
 GROUPS = H // HALF
 BLOCKS = T // P
-X_CHUNKS = ((0, 512), (512, 768), (768, 1024))
-SCALAR_SHARE = 3
-GATHERS = ((0, 128), (128, 384), (384, 640), (640, 896), (896, 1024))
+CHUNK = 256
+VECTOR_COLUMNS = 160
+GATHERS = ((0, 128, 512), (128, 384, 768), (384, 640, 1024), (640, 896, 1024), (896, 1024, 1024))
 SCATTERS = ((0, 2), (2, 4), (4, 5), (5, 7), (7, 8))
 
 
@@ -38,72 +38,73 @@ def tile_moe_rag_glu_sigmoid_kernel(
         psum_ab = ctx.enter_context(tc.psum_pool(name="psum_ab", bufs=3))
         psum_ty = ctx.enter_context(tc.psum_pool(name="psum_ty", bufs=1))
 
-        x_bytes = keep.tile([P, T], U8, name="x_bytes", align_bytes=64)
-        nc.gpsimd.memset(x_bytes[:], 0)
-
-        def scale_plane(name, scales, passes, width, queue):
-            plane = keep.tile([P, passes, width], U8, name=name, align_bytes=64)
-            nc.vector.memset(plane[:].rearrange("p s i -> p (s i)").bitcast(I32), 0)
-            rows = scales.rearrange("e s (a r) i -> r a (e s) i", r=4)
-            for r in range(4):
-                queue.dma_start(out=plane[r:P:32].bitcast(I32), in_=rows[r].bitcast(I32))
+        def scale_plane(name, passes, width, tag):
+            plane = keep.tile([P, passes, width], U8, name=name, tag=tag, align_bytes=64)
+            nc.gpsimd.memset(plane[:].rearrange("p s i -> p (s i)").bitcast(I32), 0)
             return plane
 
+        def load_scales(plane, scales):
+            rows = scales.rearrange("e s (a r) i -> r a (e s) i", r=4)
+            for r in range(4):
+                nc.sync.dma_start(out=plane[r:P:32].bitcast(I32), in_=rows[r].bitcast(I32))
+
+        w1_plane = scale_plane("w1s", E, H, "w1s")
+        w3_plane = scale_plane("w3s", E, H, "w3s")
         identity = keep.tile([P, P], F32, name="identity")
         make_identity(nc, identity[:])
         warm = keep.tile([P, 1], F32, name="warm")
         nc.vector.memset(warm[:], 0.0)
         nc.scalar.activation(warm[:], warm[:], SIGMOID)
+        x_bytes = keep.tile([P, T], U8, name="x_bytes", align_bytes=64)
+        nc.vector.memset(x_bytes[:].bitcast(I32), 0)
 
-        w1_plane = scale_plane("w1s", w1_scales, E, H, nc.scalar)
         x_rows = xT.rearrange("(p j) w -> p j w", j=4)
-        x_raw = []
-        for c0, c1 in X_CHUNKS:
-            raw = keep.tile([P, 4, c1 - c0], F32, name="raw%d" % c0)
-            nc.sync.dma_start(out=raw[:], in_=x_rows[:, :, c0:c1])
-            x_raw.append(raw)
-        offsets = keep.tile([P, T // 16], U16, name="offsets")
-        nc.sync.dma_start(offsets[:], offs)
-        w3_plane = scale_plane("w3s", w3_scales, E, H, nc.sync)
-
-        w1_sb, w3_sb = [], []
-        gate_sb = keep.tile([P, T], F32, name="gate_sb")
-        w2_sb = keep.tile([P, E * GROUPS, 2 * N], U8, name="w2_sb", align_bytes=64)
-        for e in range(E):
-            for dst, src, name in ((w1_sb, w1_words, "w1_%d"), (w3_sb, w3_words, "w3_%d")):
-                words = keep.tile([P, 2 * H], U8, name=name % e, align_bytes=64)
-                nc.sync.dma_start(out=words[:].bitcast(I32), in_=src[e, 0].bitcast(I32))
-                dst.append(words)
-            if e == 0:
-                w2_plane = scale_plane("w2s", w2_scales, E * GROUPS, N, nc.sync)
-                nc.sync.dma_start(
-                    out=w2_sb[:].bitcast(I32), in_=w2_words.rearrange("e s p n -> p (e s) n").bitcast(I32)
-                )
-                nc.sync.dma_start(out=gate_sb[:], in_=gate)
-
         x_words = keep.tile([P, T], U32, name="x_words", align_bytes=64)
-        for raw, (c0, c1) in zip(x_raw, X_CHUNKS):
-            width = c1 - c0
-            cut = width - width * SCALAR_SHARE // 8
-            side = keep.tile([P, width, 4], BF16, name="side%d" % c0, align_bytes=64)
+
+        def ring(shape, dtype, name):
+            return keep.tile(shape, dtype, name=name, tag="ring", bufs=2, align_bytes=64)
+
+        def load_x(c):
+            raw = ring([P, 4, CHUNK], F32, "raw%d" % c)
+            nc.sync.dma_start(out=raw[:], in_=x_rows[:, :, c * CHUNK : (c + 1) * CHUNK])
+            return raw
+
+        def quantise_x(c, raw, cut):
+            side = keep.tile([P, CHUNK, 4], BF16, name="side%d" % c, tag="side%d" % c, align_bytes=64)
             view = raw[:].rearrange("p j w -> p w j")
-            nc.vector.tensor_copy(out=side[:, :cut, :], in_=view[:, :cut, :])
+            if cut > 0:
+                nc.vector.tensor_copy(out=side[:, :cut, :], in_=view[:, :cut, :])
             nc.scalar.copy(out=side[:, cut:, :], in_=view[:, cut:, :])
             nc.vector.quantize_mx(
-                out=x_words[:, c0:c1].bitcast(FP8X4),
-                scales=x_bytes[:, c0:c1],
+                out=x_words[:, c * CHUNK : (c + 1) * CHUNK].bitcast(FP8X4),
+                scales=x_bytes[:, c * CHUNK : (c + 1) * CHUNK],
                 in_=side[:].rearrange("p w j -> p (w j)"),
             )
+
+        raw0 = load_x(0)
+        offsets = keep.tile([P, T // 16], U16, name="offsets")
+        nc.sync.dma_start(offsets[:], offs)
+        raw1 = load_x(1)
+        w1_first = keep.tile([P, 2 * H], U8, name="w1_first", align_bytes=64)
+        nc.sync.dma_start(out=w1_first[:].bitcast(I32), in_=w1_words[0, 0].bitcast(I32))
+        w3_first = keep.tile([P, 2 * H], U8, name="w3_first", align_bytes=64)
+        nc.sync.dma_start(out=w3_first[:].bitcast(I32), in_=w3_words[0, 0].bitcast(I32))
+        load_scales(w1_plane, w1_scales)
+        load_scales(w3_plane, w3_scales)
+        quantise_x(0, raw0, VECTOR_COLUMNS)
+        quantise_x(1, raw1, VECTOR_COLUMNS)
+        raw2 = load_x(2)
+        raw3 = load_x(3)
 
         slot_words, slot_bytes = {}, {}
 
         def gather(g):
-            s0, s1 = GATHERS[g]
+            s0, s1, reach = GATHERS[g]
             listed = offsets[:, s0 // 16 : s1 // 16]
             words = keep.tile([P, s1 - s0], U32, name="slot_words%d" % g, align_bytes=64)
-            nc.vector.tensor_copy(words[:], x_words[:].indirect(listed))
+            nc.vector.tensor_copy(words[:], x_words[:, :reach].indirect(listed))
             scale = keep.tile([P, s1 - s0], U8, name="slot_bytes%d" % g, align_bytes=64)
-            nc.vector.tensor_copy(scale[:], x_bytes[:].indirect(listed))
+            nc.vector.tensor_copy(scale[:], x_bytes[:, :reach].indirect(listed))
             for s in range(s0, s1, P):
                 slot_words[s // P] = words[:, s - s0 : s - s0 + P]
                 slot_bytes[s // P] = scale[:, s - s0 : s - s0 + P]
@@ -183,9 +184,23 @@ def tile_moe_rag_glu_sigmoid_kernel(
                     outT[:].indirect(listed), results[:], gate_sb[:, first * P : last * P], MULT
                 )
 
+        w1_sb, w3_sb = [w1_first], [w3_first]
         gather(0)
+        quantise_x(2, raw2, 0)
         first_layer(0)
         gather(1)
+        quantise_x(3, raw3, 0)
+        late = ring([P, 4 * H + E * GROUPS * 2 * N], U8, "late")
+        w2_sb = late[:, 4 * H :].rearrange("p (s n) -> p s n", n=2 * N)
+        nc.sync.dma_start(out=w2_sb.bitcast(I32), in_=w2_words.rearrange("e s p n -> p (e s) n").bitcast(I32))
+        w2_plane = scale_plane("w2s", E * GROUPS, N, "side1")
+        load_scales(w2_plane, w2_scales)
+        gate_sb = ring([P, T], F32, "gate_sb")
+        nc.sync.dma_start(out=gate_sb[:], in_=gate)
+        nc.sync.dma_start(out=late[:, : 2 * H].bitcast(I32), in_=w1_words[1, 0].bitcast(I32))
+        nc.sync.dma_start(out=late[:, 2 * H : 4 * H].bitcast(I32), in_=w3_words[1, 0].bitcast(I32))
+        w1_sb.append(late[:, : 2 * H])
+        w3_sb.append(late[:, 2 * H : 4 * H])
         first_layer(1)
         turn(0)
         gather(2)

@@ -1,7 +1,6 @@
 from contextlib import ExitStack
 
 import concourse.mybir as mybir
-from concourse.masks import make_identity
 
 K, T, E, H, N = 512, 1024, 2, 1024, 128
 COUNTS = (640, 384)
@@ -35,23 +34,17 @@ def tile_moe_rag_glu_sigmoid_kernel(
     with ExitStack() as ctx:
         keep = ctx.enter_context(tc.tile_pool(name="keep", bufs=1))
         work = ctx.enter_context(tc.tile_pool(name="work", bufs=3))
-        psum_ab = ctx.enter_context(tc.psum_pool(name="psum_ab", bufs=3))
-        psum_ty = ctx.enter_context(tc.psum_pool(name="psum_ty", bufs=1))
+        psum = ctx.enter_context(tc.psum_pool(name="psum", bufs=3))
 
-        def scale_plane(name, passes, width, tag):
-            plane = keep.tile([P, passes, width], U8, name=name, tag=tag, align_bytes=64)
-            nc.gpsimd.memset(plane[:].rearrange("p s i -> p (s i)").bitcast(I32), 0)
-            return plane
-
-        def load_scales(plane, scales):
-            rows = scales.rearrange("e s (a r) i -> r a (e s) i", r=4)
-            for r in range(4):
-                nc.sync.dma_start(out=plane[r:P:32].bitcast(I32), in_=rows[r].bitcast(I32))
-
-        w1_plane = scale_plane("w1s", E, H, "w1s")
-        w3_plane = scale_plane("w3s", E, H, "w3s")
-        identity = keep.tile([P, P], F32, name="identity")
-        make_identity(nc, identity[:])
+        scale_rows = keep.tile([P, 2, H], U8, name="scale_rows", align_bytes=64)
+        for m, scales in enumerate((w1_scales, w3_scales)):
+            nc.sync.dma_start(
+                out=scale_rows[:32, m, :].bitcast(I32), in_=scales.rearrange("e s q i -> (e s q) i").bitcast(I32)
+            )
+        for p0, p1 in ((32, 64), (64, P)):
+            nc.gpsimd.memset(scale_rows[p0:p1].rearrange("p m i -> p (m i)").bitcast(I32), 0)
+        first_planes = keep.tile([P, 2 * H], U8, name="first_planes", align_bytes=64)
+        nc.gpsimd.memset(first_planes[:].bitcast(I32), 0)
         warm = keep.tile([P, 1], F32, name="warm")
         nc.vector.memset(warm[:], 0.0)
         nc.scalar.activation(warm[:], warm[:], SIGMOID)
@@ -62,7 +55,7 @@ def tile_moe_rag_glu_sigmoid_kernel(
         x_words = keep.tile([P, T], U32, name="x_words", align_bytes=64)
 
         def ring(shape, dtype, name):
-            return keep.tile(shape, dtype, name=name, tag="ring", bufs=2, align_bytes=64)
+            return keep.tile(shape, dtype, name=name, tag="ring", bufs=3, align_bytes=64)
 
         def load_x(c):
             raw = ring([P, 4, CHUNK], F32, "raw%d" % c)
@@ -81,19 +74,47 @@ def tile_moe_rag_glu_sigmoid_kernel(
                 in_=side[:].rearrange("p w j -> p (w j)"),
             )
 
+        def load_words(m, e):
+            words = keep.tile([P, 2 * H], U8, name="loaded%d%d" % (m, e), tag="loaded%d" % m, align_bytes=64)
+            nc.sync.dma_start(out=words[:].bitcast(I32), in_=(w1_words, w3_words)[m][e, 0].bitcast(I32))
+            return words
+
+        stationary = {}
+
+        def order_words(m, e, words):
+            ordered = keep.tile([P, 2 * H], U8, name="ordered%d%d" % (m, e), align_bytes=64)
+            nc.vector.tensor_copy(
+                out=ordered[:].bitcast(U16).rearrange("p (g t q) -> p g q t", g=GROUPS, t=4),
+                in_=words[:].bitcast(U16).rearrange("p (g q t) -> p g q t", g=GROUPS, t=4),
+            )
+            stationary[m, e] = ordered
+
+        def spread_scales(queue, planes, e):
+            for r in range(4):
+                queue.dma_start(
+                    out=planes[r:P:32].bitcast(I32), in_=ordered_rows[16 * e + r : 16 * e + 16 : 4].bitcast(I32)
+                )
+
+        loaded = {(0, 0): load_words(0, 0)}
         raw0 = load_x(0)
+        loaded[1, 0] = load_words(1, 0)
         offsets = keep.tile([P, T // 16], U16, name="offsets")
         nc.sync.dma_start(offsets[:], offs)
         raw1 = load_x(1)
-        w1_first = keep.tile([P, 2 * H], U8, name="w1_first", align_bytes=64)
-        nc.sync.dma_start(out=w1_first[:].bitcast(I32), in_=w1_words[0, 0].bitcast(I32))
-        w3_first = keep.tile([P, 2 * H], U8, name="w3_first", align_bytes=64)
-        nc.sync.dma_start(out=w3_first[:].bitcast(I32), in_=w3_words[0, 0].bitcast(I32))
-        load_scales(w1_plane, w1_scales)
-        load_scales(w3_plane, w3_scales)
-        quantise_x(0, raw0, VECTOR_COLUMNS)
-        quantise_x(1, raw1, VECTOR_COLUMNS)
         raw2 = load_x(2)
+
+        ordered_rows = keep.tile([P, 2 * H], U8, name="ordered_rows", align_bytes=64)
+        nc.vector.tensor_copy(
+            out=ordered_rows[:].rearrange("p (x t q) -> p x q t", t=4, q=P),
+            in_=scale_rows[:].rearrange("p m (g q t) -> p (m g) q t", g=GROUPS, t=4),
+        )
+        spread_scales(nc.scalar, first_planes[:], 0)
+        order_words(0, 0, loaded[0, 0])
+        order_words(1, 0, loaded[1, 0])
+        quantise_x(0, raw0, 0)
+        quantise_x(1, raw1, VECTOR_COLUMNS)
+        loaded[0, 1] = load_words(0, 1)
+        loaded[1, 1] = load_words(1, 1)
         raw3 = load_x(3)
 
         slot_words, slot_bytes = {}, {}
@@ -113,47 +134,35 @@ def tile_moe_rag_glu_sigmoid_kernel(
 
         def first_layer(b):
             e = 0 if b * P < COUNTS[0] else 1
-            h_rows = work.tile([P, GROUPS, HALF], BF16, name="h_rows", align_bytes=64)
+            quads = work.tile([P, GROUPS, HALF], BF16, name="quads", align_bytes=64)
             for g in range(GROUPS):
                 banks = []
-                for words, plane, tag in ((w1_sb[e], w1_plane, "a"), (w3_sb[e], w3_plane, "b")):
-                    bank = psum_ab.tile([P, HALF], F32, name=tag)
-                    nc.tensor.matmul_mx(
-                        out=bank[:],
-                        lhsT=slot_words[b].bitcast(FP8X4),
-                        lhsT_scale=slot_bytes[b],
-                        rhs=words[:, 2 * HALF * g : 2 * HALF * (g + 1)].bitcast(FP4X4),
-                        rhs_scale=plane[:, e, HALF * g : HALF * (g + 1)],
-                        start=True,
-                        stop=True,
-                    )
-                    banks.append(bank[:].rearrange("s (p u d) -> s u p d", u=2, d=2))
-                gated = work.tile([P, HALF], F32, name="gated")
-                gated_view = gated[:].rearrange("s (u p d) -> s u p d", u=2, d=2)
-                nc.scalar.activation(gated_view, banks[0], SIGMOID)
-                nc.vector.tensor_tensor(
-                    h_rows[:, g, :].rearrange("s (u p d) -> s u p d", u=2, d=2), banks[1], gated_view, MULT
-                )
-            hidden[b] = h_rows
+                for m, tag in enumerate("ab"):
+                    bank = psum.tile([P, 4, P], F32, name=tag)
+                    for t in range(4):
+                        at = HALF * g + P * t
+                        nc.tensor.matmul_mx(
+                            out=bank[:, t, :],
+                            lhsT=stationary[m, e][:, 2 * at : 2 * (at + P)].bitcast(FP4X4),
+                            lhsT_scale=planes[e][:, m * H + at : m * H + at + P],
+                            rhs=slot_words[b].bitcast(FP8X4),
+                            rhs_scale=slot_bytes[b],
+                            start=True,
+                            stop=True,
+                        )
+                    banks.append(bank[:].rearrange("p t s -> p s t"))
+                gated = work.tile([P, P, 4], F32, name="gated")
+                nc.scalar.activation(gated[:], banks[0], SIGMOID)
+                nc.vector.tensor_tensor(quads[:, g, :].rearrange("p (s t) -> p s t", t=4), banks[1], gated[:], MULT)
+            hidden[b] = quads
 
-        def turn(b):
-            words = hidden[b][:].rearrange("s g c -> s (g c)").bitcast(F32)
-            turned = psum_ty.tile([P, GROUPS, 2, P], F32, name="turned")
-            for g in range(GROUPS):
-                for u in range(2):
-                    at = (2 * g + u) * P
-                    nc.tensor.transpose(turned[:, g, u, :], words[:, at : at + P], identity[:])
-            quads = work.tile([P, GROUPS * P * 4], BF16, name="quads", align_bytes=64)
-            nc.scalar.copy(
-                out=quads[:].bitcast(F32).rearrange("p (g s u) -> p g s u", g=GROUPS, u=2),
-                in_=turned[:].rearrange("p g u s -> p g s u"),
-            )
+        def quantise_h(b):
             codes = work.tile([P, GROUPS, P], U32, name="codes", align_bytes=64)
             scale = work.tile([P, GROUPS, P], U8, name="scale", align_bytes=64)
             nc.vector.quantize_mx(
                 out=codes[:].rearrange("p g s -> p (g s)").bitcast(FP8X4),
                 scales=scale[:].rearrange("p g s -> p (g s)"),
-                in_=quads[:],
+                in_=hidden[b][:].rearrange("p g c -> p (g c)"),
             )
             h_codes[b], h_bytes[b] = codes, scale
 
@@ -163,13 +172,14 @@ def tile_moe_rag_glu_sigmoid_kernel(
             e = 0 if b * P < COUNTS[0] else 1
             first, last = [s for s in SCATTERS if s[0] <= b < s[1]][0]
             if b == first:
-                y_banks[first] = psum_ty.tile([P, 2 * P], F32, name="y")
+                y_banks[first] = psum.tile([P, 2 * P], F32, name="y", bufs=2)
             y = y_banks[first]
             for g in range(GROUPS):
+                at = (e * GROUPS + g) * N
                 nc.tensor.matmul_mx(
                     out=y[:, (b - first) * P : (b - first + 1) * P],
                     lhsT=w2_sb[:, e * GROUPS + g, :].bitcast(FP4X4),
-                    lhsT_scale=w2_plane[:, e * GROUPS + g, :],
+                    lhsT_scale=w2_plane[:, at : at + N],
                     rhs=h_codes[b][:, g, :].bitcast(FP8X4),
                     rhs_scale=h_bytes[b][:, g, :],
                     start=(g == 0),
@@ -184,27 +194,32 @@ def tile_moe_rag_glu_sigmoid_kernel(
                     outT[:].indirect(listed), results[:], gate_sb[:, first * P : last * P], MULT
                 )
 
-        w1_sb, w3_sb = [w1_first], [w3_first]
         gather(0)
+        late_planes = keep.tile([P, 2 * H + E * GROUPS * N], U8, name="late_planes", tag="side1", align_bytes=64)
+        nc.vector.memset(late_planes[:].bitcast(I32), 0)
+        planes = (first_planes, late_planes)
+        w2_plane = late_planes[:, 2 * H :]
         quantise_x(2, raw2, 0)
         first_layer(0)
         gather(1)
-        quantise_x(3, raw3, 0)
-        late = ring([P, 4 * H + E * GROUPS * 2 * N], U8, "late")
-        w2_sb = late[:, 4 * H :].rearrange("p (s n) -> p s n", n=2 * N)
-        nc.sync.dma_start(out=w2_sb.bitcast(I32), in_=w2_words.rearrange("e s p n -> p (e s) n").bitcast(I32))
-        w2_plane = scale_plane("w2s", E * GROUPS, N, "side1")
-        load_scales(w2_plane, w2_scales)
+        w2_sb = ring([P, E * GROUPS, 2 * N], U8, "w2_sb")
+        nc.sync.dma_start(out=w2_sb[:].bitcast(I32), in_=w2_words.rearrange("e s p n -> p (e s) n").bitcast(I32))
+        w2_rows = w2_scales.rearrange("e s (a r) n -> r a (e s) n", r=4)
+        for r in range(4):
+            nc.sync.dma_start(
+                out=w2_plane[r:P:32].rearrange("p (s n) -> p s n", n=N).bitcast(I32), in_=w2_rows[r].bitcast(I32)
+            )
         gate_sb = ring([P, T], F32, "gate_sb")
         nc.sync.dma_start(out=gate_sb[:], in_=gate)
-        nc.sync.dma_start(out=late[:, : 2 * H].bitcast(I32), in_=w1_words[1, 0].bitcast(I32))
-        nc.sync.dma_start(out=late[:, 2 * H : 4 * H].bitcast(I32), in_=w3_words[1, 0].bitcast(I32))
-        w1_sb.append(late[:, : 2 * H])
-        w3_sb.append(late[:, 2 * H : 4 * H])
+        spread_scales(nc.sync, late_planes[:, : 2 * H], 1)
         first_layer(1)
-        turn(0)
+        quantise_h(0)
+        quantise_x(3, raw3, 0)
         gather(2)
         for b in range(2, BLOCKS + 2):
+            if b == 3:
+                order_words(0, 1, loaded[0, 1])
+                order_words(1, 1, loaded[1, 1])
             if b == 4:
                 gather(3)
             if b == 6:
@@ -212,6 +227,6 @@ def tile_moe_rag_glu_sigmoid_kernel(
             if b < BLOCKS:
                 first_layer(b)
             if b - 1 < BLOCKS:
-                turn(b - 1)
+                quantise_h(b - 1)
             second_layer(b - 2)
         nc.sync.dma_start(out=out, in_=outT[:])

@@ -22,9 +22,9 @@ HALF = 512
 GROUPS = H // HALF
 BLOCKS = T // P
 CHUNK = 256
-VECTOR_COLUMNS = 160
-GATHERS = ((0, 128, 512), (128, 384, 768), (384, 640, 1024), (640, 896, 1024), (896, 1024, 1024))
-SCATTERS = ((0, 2), (2, 4), (4, 5), (5, 7), (7, 8))
+VECTOR_COLUMNS = (160, 160, 160, 0)
+VECTOR_SLOTS = 48
+BANKS = (2, 4)
 
 
 def tile_moe_rag_glu_sigmoid_kernel(
@@ -41,53 +41,51 @@ def tile_moe_rag_glu_sigmoid_kernel(
             nc.sync.dma_start(
                 out=scale_rows[:32, m, :].bitcast(I32), in_=scales.rearrange("e s q i -> (e s q) i").bitcast(I32)
             )
-        for p0, p1 in ((32, 64), (64, P)):
-            nc.gpsimd.memset(scale_rows[p0:p1].rearrange("p m i -> p (m i)").bitcast(I32), 0)
-        first_planes = keep.tile([P, 2 * H], U8, name="first_planes", align_bytes=64)
-        nc.gpsimd.memset(first_planes[:].bitcast(I32), 0)
         warm = keep.tile([P, 1], F32, name="warm")
         nc.vector.memset(warm[:], 0.0)
         nc.scalar.activation(warm[:], warm[:], SIGMOID)
+        for p0, p1 in ((32, 64), (64, P)):
+            nc.vector.memset(scale_rows[p0:p1].rearrange("p m i -> p (m i)").bitcast(I32), 0)
+        first_planes = keep.tile([P, 2 * H], U8, name="first_planes", align_bytes=64)
+        nc.vector.memset(first_planes[:].bitcast(I32), 0)
         x_bytes = keep.tile([P, T], U8, name="x_bytes", align_bytes=64)
         nc.vector.memset(x_bytes[:].bitcast(I32), 0)
 
         x_rows = xT.rearrange("(p j) w -> p j w", j=4)
         x_words = keep.tile([P, T], U32, name="x_words", align_bytes=64)
 
-        def ring(shape, dtype, name):
-            return keep.tile(shape, dtype, name=name, tag="ring", bufs=3, align_bytes=64)
-
-        def load_x(c):
-            raw = ring([P, 4, CHUNK], F32, "raw%d" % c)
+        def load_x(c, tag):
+            raw = keep.tile([P, 4, CHUNK], F32, name="raw%d" % c, tag=tag, align_bytes=64)
             nc.sync.dma_start(out=raw[:], in_=x_rows[:, :, c * CHUNK : (c + 1) * CHUNK])
             return raw
 
-        def quantise_x(c, raw, cut):
+        def quantise_x(c, raw):
+            cut = VECTOR_COLUMNS[c]
             side = keep.tile([P, CHUNK, 4], BF16, name="side%d" % c, tag="side%d" % c, align_bytes=64)
             view = raw[:].rearrange("p j w -> p w j")
             if cut > 0:
                 nc.vector.tensor_copy(out=side[:, :cut, :], in_=view[:, :cut, :])
-            nc.scalar.copy(out=side[:, cut:, :], in_=view[:, cut:, :])
+            if cut < CHUNK:
+                nc.scalar.copy(out=side[:, cut:, :], in_=view[:, cut:, :])
             nc.vector.quantize_mx(
                 out=x_words[:, c * CHUNK : (c + 1) * CHUNK].bitcast(FP8X4),
                 scales=x_bytes[:, c * CHUNK : (c + 1) * CHUNK],
                 in_=side[:].rearrange("p w j -> p (w j)"),
             )
 
-        def load_words(m, e):
-            words = keep.tile([P, 2 * H], U8, name="loaded%d%d" % (m, e), tag="loaded%d" % m, align_bytes=64)
-            nc.sync.dma_start(out=words[:].bitcast(I32), in_=(w1_words, w3_words)[m][e, 0].bitcast(I32))
+        def load_words(m):
+            words = keep.tile([P, E, 2 * H], U8, name="loaded%d" % m, tag="loaded%d" % m, align_bytes=64)
+            source = (w1_words, w3_words)[m].rearrange("e s p i -> p (e s) i")
+            nc.sync.dma_start(out=words[:].bitcast(I32), in_=source.bitcast(I32))
             return words
 
-        stationary = {}
-
-        def order_words(m, e, words):
-            ordered = keep.tile([P, 2 * H], U8, name="ordered%d%d" % (m, e), align_bytes=64)
+        def order_words(m, words):
+            ordered = keep.tile([P, E, 2 * H], U8, name="ordered%d" % m, align_bytes=64)
             nc.vector.tensor_copy(
-                out=ordered[:].bitcast(U16).rearrange("p (g t q) -> p g q t", g=GROUPS, t=4),
-                in_=words[:].bitcast(U16).rearrange("p (g q t) -> p g q t", g=GROUPS, t=4),
+                out=ordered[:].bitcast(U16).rearrange("p e (g t q) -> p (e g) q t", t=4, q=P),
+                in_=words[:].bitcast(U16).rearrange("p e (g q t) -> p (e g) q t", t=4, q=P),
             )
-            stationary[m, e] = ordered
+            return ordered
 
         def spread_scales(queue, planes, e):
             for r in range(4):
@@ -95,13 +93,10 @@ def tile_moe_rag_glu_sigmoid_kernel(
                     out=planes[r:P:32].bitcast(I32), in_=ordered_rows[16 * e + r : 16 * e + 16 : 4].bitcast(I32)
                 )
 
-        loaded = {(0, 0): load_words(0, 0)}
-        raw0 = load_x(0)
-        loaded[1, 0] = load_words(1, 0)
+        loaded = [load_words(m) for m in range(2)]
         offsets = keep.tile([P, T // 16], U16, name="offsets")
         nc.sync.dma_start(offsets[:], offs)
-        raw1 = load_x(1)
-        raw2 = load_x(2)
+        raws = [load_x(c, "raw%d" % c) for c in range(2)]
 
         ordered_rows = keep.tile([P, 2 * H], U8, name="ordered_rows", align_bytes=64)
         nc.vector.tensor_copy(
@@ -109,52 +104,57 @@ def tile_moe_rag_glu_sigmoid_kernel(
             in_=scale_rows[:].rearrange("p m (g q t) -> p (m g) q t", g=GROUPS, t=4),
         )
         spread_scales(nc.scalar, first_planes[:], 0)
-        order_words(0, 0, loaded[0, 0])
-        order_words(1, 0, loaded[1, 0])
-        quantise_x(0, raw0, 0)
-        quantise_x(1, raw1, VECTOR_COLUMNS)
-        loaded[0, 1] = load_words(0, 1)
-        loaded[1, 1] = load_words(1, 1)
-        raw3 = load_x(3)
+        stationary = [order_words(m, loaded[m]) for m in range(2)]
+        raws.extend(load_x(2 + m, "loaded%d" % m) for m in range(2))
+        quantise_x(0, raws[0])
+        quantise_x(1, raws[1])
 
         slot_words, slot_bytes = {}, {}
 
-        def gather(g):
-            s0, s1, reach = GATHERS[g]
-            listed = offsets[:, s0 // 16 : s1 // 16]
-            words = keep.tile([P, s1 - s0], U32, name="slot_words%d" % g, align_bytes=64)
+        def expert(b):
+            return 0 if b * P < COUNTS[0] else 1
+
+        def gather(first, last):
+            reach = max((b + 1) * P - sum(COUNTS[: expert(b)]) + T - COUNTS[expert(b)] for b in range(first, last))
+            listed = offsets[:, first * P // 16 : last * P // 16]
+            words = keep.tile([P, (last - first) * P], U32, name="slot_words%d" % first, align_bytes=64)
             nc.vector.tensor_copy(words[:], x_words[:, :reach].indirect(listed))
-            scale = keep.tile([P, s1 - s0], U8, name="slot_bytes%d" % g, align_bytes=64)
+            scale = keep.tile([P, (last - first) * P], U8, name="slot_bytes%d" % first, align_bytes=64)
             nc.vector.tensor_copy(scale[:], x_bytes[:, :reach].indirect(listed))
-            for s in range(s0, s1, P):
-                slot_words[s // P] = words[:, s - s0 : s - s0 + P]
-                slot_bytes[s // P] = scale[:, s - s0 : s - s0 + P]
+            for b in range(first, last):
+                slot_words[b] = words[:, (b - first) * P : (b - first + 1) * P]
+                slot_bytes[b] = scale[:, (b - first) * P : (b - first + 1) * P]
 
-        hidden, h_codes, h_bytes, y_banks = {}, {}, {}, {}
+        hidden, h_codes, h_bytes, results = {}, {}, {}, {}
 
-        def first_layer(b):
-            e = 0 if b * P < COUNTS[0] else 1
-            quads = work.tile([P, GROUPS, HALF], BF16, name="quads", align_bytes=64)
-            for g in range(GROUPS):
-                banks = []
-                for m, tag in enumerate("ab"):
-                    bank = psum.tile([P, 4, P], F32, name=tag)
-                    for t in range(4):
-                        at = HALF * g + P * t
-                        nc.tensor.matmul_mx(
-                            out=bank[:, t, :],
-                            lhsT=stationary[m, e][:, 2 * at : 2 * (at + P)].bitcast(FP4X4),
-                            lhsT_scale=planes[e][:, m * H + at : m * H + at + P],
-                            rhs=slot_words[b].bitcast(FP8X4),
-                            rhs_scale=slot_bytes[b],
-                            start=True,
-                            stop=True,
-                        )
-                    banks.append(bank[:].rearrange("p t s -> p s t"))
-                gated = work.tile([P, P, 4], F32, name="gated")
-                nc.scalar.activation(gated[:], banks[0], SIGMOID)
-                nc.vector.tensor_tensor(quads[:, g, :].rearrange("p (s t) -> p s t", t=4), banks[1], gated[:], MULT)
-            hidden[b] = quads
+        def first_layer(b, g):
+            e = expert(b)
+            if g == 0:
+                hidden[b] = work.tile([P, GROUPS, HALF], BF16, name="quads", bufs=1, align_bytes=64)
+            banks = []
+            for m, tag in enumerate("ab"):
+                bank = psum.tile([P, 4, P], F32, name=tag, bufs=BANKS[m])
+                for t in range(4):
+                    at = HALF * g + P * t
+                    nc.tensor.matmul_mx(
+                        out=bank[:, t, :],
+                        lhsT=stationary[m][:, e, 2 * at : 2 * (at + P)].bitcast(FP4X4),
+                        lhsT_scale=planes[e][:, m * H + at : m * H + at + P],
+                        rhs=slot_words[b].bitcast(FP8X4),
+                        rhs_scale=slot_bytes[b],
+                        start=True,
+                        stop=True,
+                    )
+                banks.append(bank[:].rearrange("p t s -> p s t"))
+            gated = work.tile([P, P, 4], F32, name="gated", bufs=4)
+            nc.scalar.activation(gated[:], banks[0], SIGMOID)
+            h_view = hidden[b][:, g, :].rearrange("p (s t) -> p s t", t=4)
+            cut = P if g == 0 or b == 0 else VECTOR_SLOTS
+            if cut < P:
+                linear = work.tile([P, P - cut, 4], F32, name="linear")
+                nc.scalar.copy(out=linear[:], in_=banks[1][:, cut:, :])
+                nc.gpsimd.tensor_tensor(h_view[:, cut:, :], linear[:], gated[:, cut:, :], MULT)
+            nc.vector.tensor_tensor(h_view[:, :cut, :], banks[1][:, :cut, :], gated[:, :cut, :], MULT)
 
         def quantise_h(b):
             codes = work.tile([P, GROUPS, P], U32, name="codes", align_bytes=64)
@@ -169,15 +169,12 @@ def tile_moe_rag_glu_sigmoid_kernel(
         outT = keep.tile([P, T], F32, name="outT")
 
         def second_layer(b):
-            e = 0 if b * P < COUNTS[0] else 1
-            first, last = [s for s in SCATTERS if s[0] <= b < s[1]][0]
-            if b == first:
-                y_banks[first] = psum.tile([P, 2 * P], F32, name="y", bufs=2)
-            y = y_banks[first]
+            e = expert(b)
+            y = psum.tile([P, P], F32, name="y", bufs=2)
             for g in range(GROUPS):
                 at = (e * GROUPS + g) * N
                 nc.tensor.matmul_mx(
-                    out=y[:, (b - first) * P : (b - first + 1) * P],
+                    out=y[:],
                     lhsT=w2_sb[:, e * GROUPS + g, :].bitcast(FP4X4),
                     lhsT_scale=w2_plane[:, at : at + N],
                     rhs=h_codes[b][:, g, :].bitcast(FP8X4),
@@ -185,48 +182,42 @@ def tile_moe_rag_glu_sigmoid_kernel(
                     start=(g == 0),
                     stop=(g == GROUPS - 1),
                 )
-            if b == last - 1:
-                width = (last - first) * P
-                results = work.tile([P, width], F32, name="results%d" % width)
-                nc.scalar.copy(out=results[:], in_=y[:, :width])
-                listed = offsets[:, first * P // 16 : last * P // 16]
-                nc.vector.tensor_tensor(
-                    outT[:].indirect(listed), results[:], gate_sb[:, first * P : last * P], MULT
-                )
+            results[b] = work.tile([P, P], F32, name="results")
+            nc.scalar.copy(out=results[b][:], in_=y[:])
 
-        gather(0)
-        late_planes = keep.tile([P, 2 * H + E * GROUPS * N], U8, name="late_planes", tag="side1", align_bytes=64)
-        nc.vector.memset(late_planes[:].bitcast(I32), 0)
+        def scatter(b):
+            listed = offsets[:, b * P // 16 : (b + 1) * P // 16]
+            nc.vector.tensor_tensor(outT[:].indirect(listed), results[b][:], gate_sb[:, b * P : (b + 1) * P], MULT)
+
+        gather(0, 1)
+        quantise_x(2, raws[2])
+        gather(1, 3)
+        gather(5, 6)
+        quantise_x(3, raws[3])
+        gather(3, 5)
+        gather(6, 8)
+        gate_sb = keep.tile([P, T], F32, name="gate_sb", tag="raw0", align_bytes=64)
+        nc.sync.dma_start(out=gate_sb[:], in_=gate)
+        late = keep.tile([P, 2 * H + 3 * E * GROUPS * N], U8, name="late", tag="raw1", align_bytes=64)
+        nc.vector.memset(late[:, : 2 * H + E * GROUPS * N].bitcast(I32), 0)
+        late_planes = late[:, : 2 * H]
+        w2_plane = late[:, 2 * H : 2 * H + E * GROUPS * N]
+        w2_sb = late[:, 2 * H + E * GROUPS * N :].rearrange("p (s n) -> p s n", n=2 * N)
         planes = (first_planes, late_planes)
-        w2_plane = late_planes[:, 2 * H :]
-        quantise_x(2, raw2, 0)
-        first_layer(0)
-        gather(1)
-        w2_sb = ring([P, E * GROUPS, 2 * N], U8, "w2_sb")
-        nc.sync.dma_start(out=w2_sb[:].bitcast(I32), in_=w2_words.rearrange("e s p n -> p (e s) n").bitcast(I32))
+        nc.sync.dma_start(out=w2_sb.bitcast(I32), in_=w2_words.rearrange("e s p n -> p (e s) n").bitcast(I32))
         w2_rows = w2_scales.rearrange("e s (a r) n -> r a (e s) n", r=4)
         for r in range(4):
             nc.sync.dma_start(
                 out=w2_plane[r:P:32].rearrange("p (s n) -> p s n", n=N).bitcast(I32), in_=w2_rows[r].bitcast(I32)
             )
-        gate_sb = ring([P, T], F32, "gate_sb")
-        nc.sync.dma_start(out=gate_sb[:], in_=gate)
-        spread_scales(nc.sync, late_planes[:, : 2 * H], 1)
-        first_layer(1)
-        quantise_h(0)
-        quantise_x(3, raw3, 0)
-        gather(2)
-        for b in range(2, BLOCKS + 2):
-            if b == 3:
-                order_words(0, 1, loaded[0, 1])
-                order_words(1, 1, loaded[1, 1])
-            if b == 4:
-                gather(3)
-            if b == 6:
-                gather(4)
-            if b < BLOCKS:
-                first_layer(b)
-            if b - 1 < BLOCKS:
-                quantise_h(b - 1)
-            second_layer(b - 2)
+        spread_scales(nc.sync, late_planes, 1)
+        for b in range(BLOCKS):
+            first_layer(b, 0)
+            first_layer(b, 1)
+            if b >= 2:
+                scatter(b - 2)
+            quantise_h(b)
+            second_layer(b)
+        scatter(BLOCKS - 2)
+        scatter(BLOCKS - 1)
         nc.sync.dma_start(out=out, in_=outT[:])

@@ -23,7 +23,6 @@ GROUPS = H // HALF
 BLOCKS = T // P
 CHUNK = 256
 VECTOR_COLUMNS = (160, 160, 160, 0)
-VECTOR_SLOTS = 48
 BANKS = (2, 4)
 
 
@@ -130,7 +129,7 @@ def tile_moe_rag_glu_sigmoid_kernel(
         def first_layer(b, g):
             e = expert(b)
             if g == 0:
-                hidden[b] = work.tile([P, GROUPS, HALF], BF16, name="quads", bufs=1, align_bytes=64)
+                hidden[b] = work.tile([P, GROUPS, HALF], BF16, name="quads", align_bytes=64)
             banks = []
             for m, tag in enumerate("ab"):
                 bank = psum.tile([P, 4, P], F32, name=tag, bufs=BANKS[m])
@@ -149,12 +148,7 @@ def tile_moe_rag_glu_sigmoid_kernel(
             gated = work.tile([P, P, 4], F32, name="gated", bufs=4)
             nc.scalar.activation(gated[:], banks[0], SIGMOID)
             h_view = hidden[b][:, g, :].rearrange("p (s t) -> p s t", t=4)
-            cut = P if g == 0 or b == 0 else VECTOR_SLOTS
-            if cut < P:
-                linear = work.tile([P, P - cut, 4], F32, name="linear")
-                nc.scalar.copy(out=linear[:], in_=banks[1][:, cut:, :])
-                nc.gpsimd.tensor_tensor(h_view[:, cut:, :], linear[:], gated[:, cut:, :], MULT)
-            nc.vector.tensor_tensor(h_view[:, :cut, :], banks[1][:, :cut, :], gated[:, :cut, :], MULT)
+            nc.vector.tensor_tensor(h_view, banks[1], gated[:], MULT)
 
         def quantise_h(b):
             codes = work.tile([P, GROUPS, P], U32, name="codes", align_bytes=64)
@@ -211,13 +205,14 @@ def tile_moe_rag_glu_sigmoid_kernel(
                 out=w2_plane[r:P:32].rearrange("p (s n) -> p s n", n=N).bitcast(I32), in_=w2_rows[r].bitcast(I32)
             )
         spread_scales(nc.sync, late_planes, 1)
-        for b in range(BLOCKS):
-            first_layer(b, 0)
-            first_layer(b, 1)
+        for b in range(BLOCKS + 2):
+            if b < BLOCKS:
+                first_layer(b, 0)
+            if 1 <= b <= BLOCKS:
+                quantise_h(b - 1)
+                second_layer(b - 1)
+            if b < BLOCKS:
+                first_layer(b, 1)
             if b >= 2:
                 scatter(b - 2)
-            quantise_h(b)
-            second_layer(b)
-        scatter(BLOCKS - 2)
-        scatter(BLOCKS - 1)
         nc.sync.dma_start(out=out, in_=outT[:])

@@ -22,7 +22,7 @@ HALF = 512
 GROUPS = H // HALF
 BLOCKS = T // P
 CHUNK = 256
-VECTOR_COLUMNS = (160, 160, 160, 0)
+VECTOR_COLUMNS = (0, 160, 128, 0)
 BANKS = (2, 4)
 
 
@@ -92,10 +92,12 @@ def tile_moe_rag_glu_sigmoid_kernel(
                     out=planes[r:P:32].bitcast(I32), in_=ordered_rows[16 * e + r : 16 * e + 16 : 4].bitcast(I32)
                 )
 
-        loaded = [load_words(m) for m in range(2)]
+        loaded = [load_words(0)]
         offsets = keep.tile([P, T // 16], U16, name="offsets")
         nc.sync.dma_start(offsets[:], offs)
-        raws = [load_x(c, "raw%d" % c) for c in range(2)]
+        raws = [load_x(c, "raw%d" % c) for c in range(3)]
+        loaded.append(load_words(1))
+        raws.append(load_x(3, "raw3"))
 
         ordered_rows = keep.tile([P, 2 * H], U8, name="ordered_rows", align_bytes=64)
         nc.vector.tensor_copy(
@@ -103,8 +105,17 @@ def tile_moe_rag_glu_sigmoid_kernel(
             in_=scale_rows[:].rearrange("p m (g q t) -> p (m g) q t", g=GROUPS, t=4),
         )
         spread_scales(nc.scalar, first_planes[:], 0)
-        stationary = [order_words(m, loaded[m]) for m in range(2)]
-        raws.extend(load_x(2 + m, "loaded%d" % m) for m in range(2))
+        stationary = [order_words(0, loaded[0])]
+        late_planes = keep.tile([P, 2 * H + E * GROUPS * N], U8, name="late_planes", tag="loaded0", align_bytes=64)
+        nc.vector.memset(late_planes[:].bitcast(I32), 0)
+        planes = (first_planes[:], late_planes[:, : 2 * H])
+        w2_plane = late_planes[:, 2 * H :]
+        spread_scales(nc.sync, planes[1], 1)
+        w2_rows = w2_scales.rearrange("e s (a r) n -> r a (e s) n", r=4)
+        for r in range(4):
+            nc.sync.dma_start(
+                out=w2_plane[r:P:32].rearrange("p (s n) -> p s n", n=N).bitcast(I32), in_=w2_rows[r].bitcast(I32)
+            )
         quantise_x(0, raws[0])
         quantise_x(1, raws[1])
 
@@ -185,26 +196,16 @@ def tile_moe_rag_glu_sigmoid_kernel(
 
         gather(0, 1)
         quantise_x(2, raws[2])
+        stationary.append(order_words(1, loaded[1]))
         gather(1, 3)
         gather(5, 6)
         quantise_x(3, raws[3])
         gather(3, 5)
         gather(6, 8)
-        gate_sb = keep.tile([P, T], F32, name="gate_sb", tag="raw0", align_bytes=64)
+        w2_sb = keep.tile([P, E * GROUPS, 2 * N], U8, name="w2_sb", tag="raw1", align_bytes=64)
+        nc.sync.dma_start(out=w2_sb[:].bitcast(I32), in_=w2_words.rearrange("e s p n -> p (e s) n").bitcast(I32))
+        gate_sb = keep.tile([P, T], F32, name="gate_sb", tag="raw2", align_bytes=64)
         nc.sync.dma_start(out=gate_sb[:], in_=gate)
-        late = keep.tile([P, 2 * H + 3 * E * GROUPS * N], U8, name="late", tag="raw1", align_bytes=64)
-        nc.vector.memset(late[:, : 2 * H + E * GROUPS * N].bitcast(I32), 0)
-        late_planes = late[:, : 2 * H]
-        w2_plane = late[:, 2 * H : 2 * H + E * GROUPS * N]
-        w2_sb = late[:, 2 * H + E * GROUPS * N :].rearrange("p (s n) -> p s n", n=2 * N)
-        planes = (first_planes, late_planes)
-        nc.sync.dma_start(out=w2_sb.bitcast(I32), in_=w2_words.rearrange("e s p n -> p (e s) n").bitcast(I32))
-        w2_rows = w2_scales.rearrange("e s (a r) n -> r a (e s) n", r=4)
-        for r in range(4):
-            nc.sync.dma_start(
-                out=w2_plane[r:P:32].rearrange("p (s n) -> p s n", n=N).bitcast(I32), in_=w2_rows[r].bitcast(I32)
-            )
-        spread_scales(nc.sync, late_planes, 1)
         for b in range(BLOCKS + 2):
             if b < BLOCKS:
                 first_layer(b, 0)

@@ -18,12 +18,29 @@ FP4X4 = mybir.dt.float4_e2m1fn_x4
 MULT = mybir.AluOpType.mult
 SIGMOID = mybir.ActivationFunctionType.Sigmoid
 
-HALF = 512
-GROUPS = H // HALF
+PASS = 4 * P
+GROUPS = H // PASS
+ROWS = PASS // 32
 BLOCKS = T // P
+LIST_COLUMNS = P // 16
 CHUNK = 256
-VECTOR_COLUMNS = (0, 160, 128, 0)
-BANKS = (2, 4)
+VECTOR_TOKENS = (0, 160, 128, 0)
+A_BANKS, B_BANKS, Y_BANKS = 2, 4, 2
+GATED_BUFFERS = 4
+SCATTER_LAG = 2
+EARLY_BLOCKS = 4
+
+
+def expert(b):
+    return 0 if b * P < COUNTS[0] else 1
+
+
+def first_slot(b):
+    return b * P - sum(COUNTS[: expert(b)])
+
+
+def reach(b):
+    return first_slot(b) + P + T - COUNTS[expert(b)]
 
 
 def tile_moe_rag_glu_sigmoid_kernel(
@@ -33,12 +50,13 @@ def tile_moe_rag_glu_sigmoid_kernel(
     with ExitStack() as ctx:
         keep = ctx.enter_context(tc.tile_pool(name="keep", bufs=1))
         work = ctx.enter_context(tc.tile_pool(name="work", bufs=3))
-        psum = ctx.enter_context(tc.psum_pool(name="psum", bufs=3))
+        psum = ctx.enter_context(tc.psum_pool(name="psum", bufs=1))
 
         scale_rows = keep.tile([P, 2, H], U8, name="scale_rows", align_bytes=64)
         for m, scales in enumerate((w1_scales, w3_scales)):
             nc.sync.dma_start(
-                out=scale_rows[:32, m, :].bitcast(I32), in_=scales.rearrange("e s q i -> (e s q) i").bitcast(I32)
+                out=scale_rows[: E * ROWS, m, :].bitcast(I32),
+                in_=scales.rearrange("e s q i -> (e s q) i").bitcast(I32),
             )
         warm = keep.tile([P, 1], F32, name="warm")
         nc.vector.memset(warm[:], 0.0)
@@ -49,23 +67,21 @@ def tile_moe_rag_glu_sigmoid_kernel(
         nc.vector.memset(first_planes[:].bitcast(I32), 0)
         x_bytes = keep.tile([P, T], U8, name="x_bytes", align_bytes=64)
         nc.vector.memset(x_bytes[:].bitcast(I32), 0)
-
-        x_rows = xT.rearrange("(p j) w -> p j w", j=4)
         x_words = keep.tile([P, T], U32, name="x_words", align_bytes=64)
+        x_rows = xT.rearrange("(p j) w -> p j w", j=4)
 
-        def load_x(c, tag):
-            raw = keep.tile([P, 4, CHUNK], F32, name="raw%d" % c, tag=tag, align_bytes=64)
+        def load_x(c):
+            raw = keep.tile([P, 4, CHUNK], F32, name="raw%d" % c, tag="raw%d" % c, align_bytes=64)
             nc.sync.dma_start(out=raw[:], in_=x_rows[:, :, c * CHUNK : (c + 1) * CHUNK])
             return raw
 
-        def quantise_x(c, raw):
-            cut = VECTOR_COLUMNS[c]
-            side = keep.tile([P, CHUNK, 4], BF16, name="side%d" % c, tag="side%d" % c, align_bytes=64)
-            view = raw[:].rearrange("p j w -> p w j")
+        def quantise_x(c):
+            cut = VECTOR_TOKENS[c]
+            side = keep.tile([P, CHUNK, 4], BF16, name="side%d" % c, align_bytes=64)
+            view = raws[c][:].rearrange("p j w -> p w j")
             if cut > 0:
                 nc.vector.tensor_copy(out=side[:, :cut, :], in_=view[:, :cut, :])
-            if cut < CHUNK:
-                nc.scalar.copy(out=side[:, cut:, :], in_=view[:, cut:, :])
+            nc.scalar.copy(out=side[:, cut:, :], in_=view[:, cut:, :])
             nc.vector.quantize_mx(
                 out=x_words[:, c * CHUNK : (c + 1) * CHUNK].bitcast(FP8X4),
                 scales=x_bytes[:, c * CHUNK : (c + 1) * CHUNK],
@@ -78,74 +94,89 @@ def tile_moe_rag_glu_sigmoid_kernel(
             nc.sync.dma_start(out=words[:].bitcast(I32), in_=source.bitcast(I32))
             return words
 
-        def order_words(m, words):
+        def order_words(m):
             ordered = keep.tile([P, E, 2 * H], U8, name="ordered%d" % m, align_bytes=64)
             nc.vector.tensor_copy(
                 out=ordered[:].bitcast(U16).rearrange("p e (g t q) -> p (e g) q t", t=4, q=P),
-                in_=words[:].bitcast(U16).rearrange("p e (g q t) -> p (e g) q t", t=4, q=P),
+                in_=loaded[m][:].bitcast(U16).rearrange("p e (g q t) -> p (e g) q t", t=4, q=P),
             )
             return ordered
 
-        def spread_scales(queue, planes, e):
+        def spread_scales(queue, e):
             for r in range(4):
                 queue.dma_start(
-                    out=planes[r:P:32].bitcast(I32), in_=ordered_rows[16 * e + r : 16 * e + 16 : 4].bitcast(I32)
+                    out=planes[e][r:P:32].bitcast(I32),
+                    in_=ordered_rows[ROWS * e + r : ROWS * (e + 1) : 4].bitcast(I32),
                 )
 
         loaded = [load_words(0)]
         offsets = keep.tile([P, T // 16], U16, name="offsets")
         nc.sync.dma_start(offsets[:], offs)
-        raws = [load_x(c, "raw%d" % c) for c in range(3)]
+        raws = [load_x(c) for c in range(3)]
         loaded.append(load_words(1))
-        raws.append(load_x(3, "raw3"))
+        raws.append(load_x(3))
 
         ordered_rows = keep.tile([P, 2 * H], U8, name="ordered_rows", align_bytes=64)
         nc.vector.tensor_copy(
             out=ordered_rows[:].rearrange("p (x t q) -> p x q t", t=4, q=P),
             in_=scale_rows[:].rearrange("p m (g q t) -> p (m g) q t", g=GROUPS, t=4),
         )
-        spread_scales(nc.scalar, first_planes[:], 0)
-        stationary = [order_words(0, loaded[0])]
+        planes = [first_planes[:]]
+        spread_scales(nc.scalar, 0)
+        stationary = [order_words(0)]
+
         late_planes = keep.tile([P, 2 * H + E * GROUPS * N], U8, name="late_planes", tag="loaded0", align_bytes=64)
         nc.vector.memset(late_planes[:].bitcast(I32), 0)
-        planes = (first_planes[:], late_planes[:, : 2 * H])
+        planes.append(late_planes[:, : 2 * H])
         w2_plane = late_planes[:, 2 * H :]
-        spread_scales(nc.sync, planes[1], 1)
+        spread_scales(nc.sync, 1)
         w2_rows = w2_scales.rearrange("e s (a r) n -> r a (e s) n", r=4)
         for r in range(4):
             nc.sync.dma_start(
                 out=w2_plane[r:P:32].rearrange("p (s n) -> p s n", n=N).bitcast(I32), in_=w2_rows[r].bitcast(I32)
             )
-        quantise_x(0, raws[0])
-        quantise_x(1, raws[1])
 
         slot_words, slot_bytes = {}, {}
 
-        def expert(b):
-            return 0 if b * P < COUNTS[0] else 1
-
         def gather(first, last):
-            reach = max((b + 1) * P - sum(COUNTS[: expert(b)]) + T - COUNTS[expert(b)] for b in range(first, last))
-            listed = offsets[:, first * P // 16 : last * P // 16]
+            bound = max(reach(b) for b in range(first, last))
+            listed = offsets[:, first * LIST_COLUMNS : last * LIST_COLUMNS]
             words = keep.tile([P, (last - first) * P], U32, name="slot_words%d" % first, align_bytes=64)
-            nc.vector.tensor_copy(words[:], x_words[:, :reach].indirect(listed))
+            nc.vector.tensor_copy(words[:], x_words[:, :bound].indirect(listed))
             scale = keep.tile([P, (last - first) * P], U8, name="slot_bytes%d" % first, align_bytes=64)
-            nc.vector.tensor_copy(scale[:], x_bytes[:, :reach].indirect(listed))
+            nc.vector.tensor_copy(scale[:], x_bytes[:, :bound].indirect(listed))
             for b in range(first, last):
                 slot_words[b] = words[:, (b - first) * P : (b - first + 1) * P]
                 slot_bytes[b] = scale[:, (b - first) * P : (b - first + 1) * P]
 
-        hidden, h_codes, h_bytes, results = {}, {}, {}, {}
+        quantise_x(0)
+        quantise_x(1)
+        gather(0, 1)
+        quantise_x(2)
+        stationary.append(order_words(1))
+        gather(1, 3)
+        gather(5, 6)
+        quantise_x(3)
+        gather(6, 8)
+        gather(3, 5)
+
+        w2_sb = keep.tile([P, E * GROUPS, 2 * N], U8, name="w2_sb", tag="raw1", align_bytes=64)
+        nc.sync.dma_start(out=w2_sb[:].bitcast(I32), in_=w2_words.rearrange("e s p n -> p (e s) n").bitcast(I32))
+        gate_sb = keep.tile([P, T], F32, name="gate_sb", tag="raw2", align_bytes=64)
+        nc.sync.dma_start(out=gate_sb[:], in_=gate)
+
+        hidden, results = {}, {}
+        outT = keep.tile([P, T], F32, name="outT")
 
         def first_layer(b, g):
             e = expert(b)
             if g == 0:
-                hidden[b] = work.tile([P, GROUPS, HALF], BF16, name="quads", align_bytes=64)
+                hidden[b] = work.tile([P, GROUPS, PASS], BF16, name="hidden", align_bytes=64)
             banks = []
-            for m, tag in enumerate("ab"):
-                bank = psum.tile([P, 4, P], F32, name=tag, bufs=BANKS[m])
+            for m, (tag, depth) in enumerate((("a", A_BANKS), ("b", B_BANKS))):
+                bank = psum.tile([P, 4, P], F32, name=tag, bufs=depth)
                 for t in range(4):
-                    at = HALF * g + P * t
+                    at = PASS * g + P * t
                     nc.tensor.matmul_mx(
                         out=bank[:, t, :],
                         lhsT=stationary[m][:, e, 2 * at : 2 * (at + P)].bitcast(FP4X4),
@@ -156,34 +187,29 @@ def tile_moe_rag_glu_sigmoid_kernel(
                         stop=True,
                     )
                 banks.append(bank[:].rearrange("p t s -> p s t"))
-            gated = work.tile([P, P, 4], F32, name="gated", bufs=4)
+            gated = work.tile([P, P, 4], F32, name="gated", bufs=GATED_BUFFERS)
             nc.scalar.activation(gated[:], banks[0], SIGMOID)
-            h_view = hidden[b][:, g, :].rearrange("p (s t) -> p s t", t=4)
-            nc.vector.tensor_tensor(h_view, banks[1], gated[:], MULT)
+            nc.vector.tensor_tensor(hidden[b][:, g, :].rearrange("p (s t) -> p s t", t=4), banks[1], gated[:], MULT)
 
-        def quantise_h(b):
+        def second_layer(b, passes_a_call):
             codes = work.tile([P, GROUPS, P], U32, name="codes", align_bytes=64)
             scale = work.tile([P, GROUPS, P], U8, name="scale", align_bytes=64)
-            nc.vector.quantize_mx(
-                out=codes[:].rearrange("p g s -> p (g s)").bitcast(FP8X4),
-                scales=scale[:].rearrange("p g s -> p (g s)"),
-                in_=hidden[b][:].rearrange("p g c -> p (g c)"),
-            )
-            h_codes[b], h_bytes[b] = codes, scale
-
-        outT = keep.tile([P, T], F32, name="outT")
-
-        def second_layer(b):
-            e = expert(b)
-            y = psum.tile([P, P], F32, name="y", bufs=2)
+            for g in range(0, GROUPS, passes_a_call):
+                taken = slice(g, g + passes_a_call)
+                nc.vector.quantize_mx(
+                    out=codes[:, taken].rearrange("p g s -> p (g s)").bitcast(FP8X4),
+                    scales=scale[:, taken].rearrange("p g s -> p (g s)"),
+                    in_=hidden[b][:, taken].rearrange("p g c -> p (g c)"),
+                )
+            y = psum.tile([P, P], F32, name="y", bufs=Y_BANKS)
             for g in range(GROUPS):
-                at = (e * GROUPS + g) * N
+                at = expert(b) * GROUPS + g
                 nc.tensor.matmul_mx(
                     out=y[:],
-                    lhsT=w2_sb[:, e * GROUPS + g, :].bitcast(FP4X4),
-                    lhsT_scale=w2_plane[:, at : at + N],
-                    rhs=h_codes[b][:, g, :].bitcast(FP8X4),
-                    rhs_scale=h_bytes[b][:, g, :],
+                    lhsT=w2_sb[:, at, :].bitcast(FP4X4),
+                    lhsT_scale=w2_plane[:, at * N : (at + 1) * N],
+                    rhs=codes[:, g, :].bitcast(FP8X4),
+                    rhs_scale=scale[:, g, :],
                     start=(g == 0),
                     stop=(g == GROUPS - 1),
                 )
@@ -191,29 +217,24 @@ def tile_moe_rag_glu_sigmoid_kernel(
             nc.scalar.copy(out=results[b][:], in_=y[:])
 
         def scatter(b):
-            listed = offsets[:, b * P // 16 : (b + 1) * P // 16]
+            listed = offsets[:, b * LIST_COLUMNS : (b + 1) * LIST_COLUMNS]
             nc.vector.tensor_tensor(outT[:].indirect(listed), results[b][:], gate_sb[:, b * P : (b + 1) * P], MULT)
 
-        gather(0, 1)
-        quantise_x(2, raws[2])
-        stationary.append(order_words(1, loaded[1]))
-        gather(1, 3)
-        gather(5, 6)
-        quantise_x(3, raws[3])
-        gather(3, 5)
-        gather(6, 8)
-        w2_sb = keep.tile([P, E * GROUPS, 2 * N], U8, name="w2_sb", tag="raw1", align_bytes=64)
-        nc.sync.dma_start(out=w2_sb[:].bitcast(I32), in_=w2_words.rearrange("e s p n -> p (e s) n").bitcast(I32))
-        gate_sb = keep.tile([P, T], F32, name="gate_sb", tag="raw2", align_bytes=64)
-        nc.sync.dma_start(out=gate_sb[:], in_=gate)
-        for b in range(BLOCKS + 2):
-            if b < BLOCKS:
-                first_layer(b, 0)
-            if 1 <= b <= BLOCKS:
-                quantise_h(b - 1)
-                second_layer(b - 1)
-            if b < BLOCKS:
-                first_layer(b, 1)
-            if b >= 2:
-                scatter(b - 2)
-        nc.sync.dma_start(out=out, in_=outT[:])
+        by_first_slot = sorted(range(BLOCKS), key=first_slot)
+        order = sorted(by_first_slot[:EARLY_BLOCKS]) + by_first_slot[EARLY_BLOCKS:]
+        early = first_slot(order[EARLY_BLOCKS])
+
+        for i in range(BLOCKS + SCATTER_LAG):
+            if i < BLOCKS:
+                first_layer(order[i], 0)
+            if 1 <= i <= BLOCKS:
+                second_layer(order[i - 1], 1 if i == BLOCKS else GROUPS)
+            if i < BLOCKS:
+                first_layer(order[i], 1)
+            if i >= SCATTER_LAG:
+                scatter(order[i - SCATTER_LAG])
+            if i - SCATTER_LAG == EARLY_BLOCKS - 1:
+                finished = keep.tile([P, early], F32, name="finished")
+                nc.scalar.copy(out=finished[:], in_=outT[:, :early])
+                nc.sync.dma_start(out=out[:, :early], in_=finished[:])
+        nc.sync.dma_start(out=out[:, early:], in_=outT[:, early:])

@@ -97,8 +97,8 @@ def tile_moe_rag_glu_sigmoid_kernel(
         def order_words(m):
             ordered = keep.tile([P, E, 2 * H], U8, name="ordered%d" % m, align_bytes=64)
             nc.vector.tensor_copy(
-                out=ordered[:].bitcast(U16).rearrange("p e (g t q) -> p (e g) q t", t=4, q=P),
-                in_=loaded[m][:].bitcast(U16).rearrange("p e (g q t) -> p (e g) q t", t=4, q=P),
+                out=ordered[:].bitcast(U16).rearrange("p e (g t q) -> p (e g) t q", t=4, q=P),
+                in_=loaded[m][:].bitcast(U16).rearrange("p e (g q t) -> p (e g) t q", t=4, q=P),
             )
             return ordered
 
@@ -118,8 +118,8 @@ def tile_moe_rag_glu_sigmoid_kernel(
 
         ordered_rows = keep.tile([P, 2 * H], U8, name="ordered_rows", align_bytes=64)
         nc.vector.tensor_copy(
-            out=ordered_rows[:].rearrange("p (x t q) -> p x q t", t=4, q=P),
-            in_=scale_rows[:].rearrange("p m (g q t) -> p (m g) q t", g=GROUPS, t=4),
+            out=ordered_rows[:].rearrange("p (x t q) -> p x t q", t=4, q=P),
+            in_=scale_rows[:].rearrange("p m (g q t) -> p (m g) t q", g=GROUPS, t=4),
         )
         planes = [first_planes[:]]
         spread_scales(nc.scalar, 0)

@@ -23,6 +23,7 @@ GROUPS = H // PASS
 ROWS = PASS // 32
 BLOCKS = T // P
 LIST_COLUMNS = P // 16
+ALIGN = 256
 CHUNK = 256
 VECTOR_TOKENS = (0, 160, 128, 0)
 A_BANKS, B_BANKS, Y_BANKS = 2, 4, 2
@@ -52,7 +53,7 @@ def tile_moe_rag_glu_sigmoid_kernel(
         work = ctx.enter_context(tc.tile_pool(name="work", bufs=3))
         psum = ctx.enter_context(tc.psum_pool(name="psum", bufs=1))
 
-        scale_rows = keep.tile([P, 2, H], U8, name="scale_rows", align_bytes=64)
+        scale_rows = keep.tile([P, 2, H], U8, name="scale_rows", align_bytes=ALIGN)
         for m, scales in enumerate((w1_scales, w3_scales)):
             nc.sync.dma_start(
                 out=scale_rows[: E * ROWS, m, :].bitcast(I32),
@@ -63,21 +64,21 @@ def tile_moe_rag_glu_sigmoid_kernel(
         nc.scalar.activation(warm[:], warm[:], SIGMOID)
         for p0, p1 in ((32, 64), (64, P)):
             nc.vector.memset(scale_rows[p0:p1].rearrange("p m i -> p (m i)").bitcast(I32), 0)
-        first_planes = keep.tile([P, 2 * H], U8, name="first_planes", align_bytes=64)
+        first_planes = keep.tile([P, 2 * H], U8, name="first_planes", align_bytes=ALIGN)
         nc.vector.memset(first_planes[:].bitcast(I32), 0)
-        x_bytes = keep.tile([P, T], U8, name="x_bytes", align_bytes=64)
+        x_bytes = keep.tile([P, T], U8, name="x_bytes", align_bytes=ALIGN)
         nc.vector.memset(x_bytes[:].bitcast(I32), 0)
-        x_words = keep.tile([P, T], U32, name="x_words", align_bytes=64)
+        x_words = keep.tile([P, T], U32, name="x_words", align_bytes=ALIGN)
         x_rows = xT.rearrange("(p j) w -> p j w", j=4)
 
         def load_x(c):
-            raw = keep.tile([P, 4, CHUNK], F32, name="raw%d" % c, tag="raw%d" % c, align_bytes=64)
+            raw = keep.tile([P, 4, CHUNK], F32, name="raw%d" % c, tag="raw%d" % c, align_bytes=ALIGN)
             nc.sync.dma_start(out=raw[:], in_=x_rows[:, :, c * CHUNK : (c + 1) * CHUNK])
             return raw
 
         def quantise_x(c):
             cut = VECTOR_TOKENS[c]
-            side = keep.tile([P, CHUNK, 4], BF16, name="side%d" % c, align_bytes=64)
+            side = keep.tile([P, CHUNK, 4], BF16, name="side%d" % c, align_bytes=ALIGN)
             view = raws[c][:].rearrange("p j w -> p w j")
             if cut > 0:
                 nc.vector.tensor_copy(out=side[:, :cut, :], in_=view[:, :cut, :])
@@ -89,13 +90,13 @@ def tile_moe_rag_glu_sigmoid_kernel(
             )
 
         def load_words(m):
-            words = keep.tile([P, E, 2 * H], U8, name="loaded%d" % m, tag="loaded%d" % m, align_bytes=64)
+            words = keep.tile([P, E, 2 * H], U8, name="loaded%d" % m, tag="loaded%d" % m, align_bytes=ALIGN)
             source = (w1_words, w3_words)[m].rearrange("e s p i -> p (e s) i")
             nc.sync.dma_start(out=words[:].bitcast(I32), in_=source.bitcast(I32))
             return words
 
         def order_words(m):
-            ordered = keep.tile([P, E, 2 * H], U8, name="ordered%d" % m, align_bytes=64)
+            ordered = keep.tile([P, E, 2 * H], U8, name="ordered%d" % m, align_bytes=ALIGN)
             nc.vector.tensor_copy(
                 out=ordered[:].bitcast(U16).rearrange("p e (g t q) -> p (e g) t q", t=4, q=P),
                 in_=loaded[m][:].bitcast(U16).rearrange("p e (g q t) -> p (e g) t q", t=4, q=P),
@@ -110,13 +111,13 @@ def tile_moe_rag_glu_sigmoid_kernel(
                 )
 
         loaded = [load_words(0)]
-        offsets = keep.tile([P, T // 16], U16, name="offsets")
+        offsets = keep.tile([P, T // 16], U16, name="offsets", align_bytes=ALIGN)
         nc.sync.dma_start(offsets[:], offs)
         raws = [load_x(c) for c in range(3)]
         loaded.append(load_words(1))
         raws.append(load_x(3))
 
-        ordered_rows = keep.tile([P, 2 * H], U8, name="ordered_rows", align_bytes=64)
+        ordered_rows = keep.tile([P, 2 * H], U8, name="ordered_rows", align_bytes=ALIGN)
         nc.vector.tensor_copy(
             out=ordered_rows[:].rearrange("p (x t q) -> p x t q", t=4, q=P),
             in_=scale_rows[:].rearrange("p m (g q t) -> p (m g) t q", g=GROUPS, t=4),
@@ -125,7 +126,7 @@ def tile_moe_rag_glu_sigmoid_kernel(
         spread_scales(nc.scalar, 0)
         stationary = [order_words(0)]
 
-        late_planes = keep.tile([P, 2 * H + E * GROUPS * N], U8, name="late_planes", tag="loaded0", align_bytes=64)
+        late_planes = keep.tile([P, 2 * H + E * GROUPS * N], U8, name="late_planes", tag="loaded0", align_bytes=ALIGN)
         nc.vector.memset(late_planes[:].bitcast(I32), 0)
         planes.append(late_planes[:, : 2 * H])
         w2_plane = late_planes[:, 2 * H :]
@@ -141,9 +142,9 @@ def tile_moe_rag_glu_sigmoid_kernel(
         def gather(first, last):
             bound = max(reach(b) for b in range(first, last))
             listed = offsets[:, first * LIST_COLUMNS : last * LIST_COLUMNS]
-            words = keep.tile([P, (last - first) * P], U32, name="slot_words%d" % first, align_bytes=64)
+            words = keep.tile([P, (last - first) * P], U32, name="slot_words%d" % first, align_bytes=ALIGN)
             nc.vector.tensor_copy(words[:], x_words[:, :bound].indirect(listed))
-            scale = keep.tile([P, (last - first) * P], U8, name="slot_bytes%d" % first, align_bytes=64)
+            scale = keep.tile([P, (last - first) * P], U8, name="slot_bytes%d" % first, align_bytes=ALIGN)
             nc.vector.tensor_copy(scale[:], x_bytes[:, :bound].indirect(listed))
             for b in range(first, last):
                 slot_words[b] = words[:, (b - first) * P : (b - first + 1) * P]
@@ -160,18 +161,18 @@ def tile_moe_rag_glu_sigmoid_kernel(
         gather(6, 8)
         gather(3, 5)
 
-        w2_sb = keep.tile([P, E * GROUPS, 2 * N], U8, name="w2_sb", tag="raw1", align_bytes=64)
+        w2_sb = keep.tile([P, E * GROUPS, 2 * N], U8, name="w2_sb", tag="raw1", align_bytes=ALIGN)
         nc.sync.dma_start(out=w2_sb[:].bitcast(I32), in_=w2_words.rearrange("e s p n -> p (e s) n").bitcast(I32))
-        gate_sb = keep.tile([P, T], F32, name="gate_sb", tag="raw2", align_bytes=64)
+        gate_sb = keep.tile([P, T], F32, name="gate_sb", tag="raw2", align_bytes=ALIGN)
         nc.sync.dma_start(out=gate_sb[:], in_=gate)
 
         hidden, results = {}, {}
-        outT = keep.tile([P, T], F32, name="outT")
+        outT = keep.tile([P, T], F32, name="outT", align_bytes=ALIGN)
 
         def first_layer(b, g):
             e = expert(b)
             if g == 0:
-                hidden[b] = work.tile([P, GROUPS, PASS], BF16, name="hidden", align_bytes=64)
+                hidden[b] = work.tile([P, GROUPS, PASS], BF16, name="hidden", align_bytes=ALIGN)
             banks = []
             for m, (tag, depth) in enumerate((("a", A_BANKS), ("b", B_BANKS))):
                 bank = psum.tile([P, 4, P], F32, name=tag, bufs=depth)
@@ -187,13 +188,13 @@ def tile_moe_rag_glu_sigmoid_kernel(
                         stop=True,
                     )
                 banks.append(bank[:].rearrange("p t s -> p s t"))
-            gated = work.tile([P, P, 4], F32, name="gated", bufs=GATED_BUFFERS)
+            gated = work.tile([P, P, 4], F32, name="gated", bufs=GATED_BUFFERS, align_bytes=ALIGN)
             nc.scalar.activation(gated[:], banks[0], SIGMOID)
             nc.vector.tensor_tensor(hidden[b][:, g, :].rearrange("p (s t) -> p s t", t=4), banks[1], gated[:], MULT)
 
         def second_layer(b, passes_a_call):
-            codes = work.tile([P, GROUPS, P], U32, name="codes", align_bytes=64)
-            scale = work.tile([P, GROUPS, P], U8, name="scale", align_bytes=64)
+            codes = work.tile([P, GROUPS, P], U32, name="codes", align_bytes=ALIGN)
+            scale = work.tile([P, GROUPS, P], U8, name="scale", align_bytes=ALIGN)
             for g in range(0, GROUPS, passes_a_call):
                 taken = slice(g, g + passes_a_call)
                 nc.vector.quantize_mx(
@@ -213,7 +214,7 @@ def tile_moe_rag_glu_sigmoid_kernel(
                     start=(g == 0),
                     stop=(g == GROUPS - 1),
                 )
-            results[b] = work.tile([P, P], F32, name="results")
+            results[b] = work.tile([P, P], F32, name="results", align_bytes=ALIGN)
             nc.scalar.copy(out=results[b][:], in_=y[:])
 
         def scatter(b):
@@ -234,7 +235,7 @@ def tile_moe_rag_glu_sigmoid_kernel(
             if i >= SCATTER_LAG:
                 scatter(order[i - SCATTER_LAG])
             if i - SCATTER_LAG == EARLY_BLOCKS - 1:
-                finished = keep.tile([P, early], F32, name="finished")
+                finished = keep.tile([P, early], F32, name="finished", align_bytes=ALIGN)
                 nc.scalar.copy(out=finished[:], in_=outT[:, :early])
                 nc.sync.dma_start(out=out[:, :early], in_=finished[:])
         nc.sync.dma_start(out=out[:, early:], in_=outT[:, early:])

@@ -79,10 +79,11 @@ def tile_moe_rag_glu_sigmoid_kernel(
         def quantise_x(c):
             cut = VECTOR_TOKENS[c]
             side = keep.tile([P, CHUNK, 4], BF16, name="side%d" % c, align_bytes=ALIGN)
-            view = raws[c][:].rearrange("p j w -> p w j")
+            source = raws[c][:].rearrange("p j (w n) -> p w j n", n=4)
+            target = side[:].rearrange("p (w n) j -> p w j n", n=4)
             if cut > 0:
-                nc.vector.tensor_copy(out=side[:, :cut, :], in_=view[:, :cut, :])
-            nc.scalar.copy(out=side[:, cut:, :], in_=view[:, cut:, :])
+                nc.vector.tensor_copy(out=target[:, : cut // 4], in_=source[:, : cut // 4])
+            nc.scalar.copy(out=target[:, cut // 4 :], in_=source[:, cut // 4 :])
             nc.vector.quantize_mx(
                 out=x_words[:, c * CHUNK : (c + 1) * CHUNK].bitcast(FP8X4),
                 scales=x_bytes[:, c * CHUNK : (c + 1) * CHUNK],

@@ -53,7 +53,7 @@ def tile_moe_rag_glu_sigmoid_kernel(
         work = ctx.enter_context(tc.tile_pool(name="work", bufs=3))
         psum = ctx.enter_context(tc.psum_pool(name="psum", bufs=1))
 
-        scale_rows = keep.tile([P, 2, H], U8, name="scale_rows", align_bytes=ALIGN)
+        scale_rows = keep.tile([P, 2, H], U8, name="scale_rows", tag="scale_rows", align_bytes=ALIGN)
         for m, scales in enumerate((w1_scales, w3_scales)):
             nc.sync.dma_start(
                 out=scale_rows[: E * ROWS, m, :].bitcast(I32),
@@ -71,8 +71,8 @@ def tile_moe_rag_glu_sigmoid_kernel(
         x_words = keep.tile([P, T], U32, name="x_words", align_bytes=ALIGN)
         x_rows = xT.rearrange("(p j) w -> p j w", j=4)
 
-        def load_x(c):
-            raw = keep.tile([P, 4, CHUNK], F32, name="raw%d" % c, tag="raw%d" % c, align_bytes=ALIGN)
+        def load_x(c, tag):
+            raw = keep.tile([P, 4, CHUNK], F32, name="raw%d" % c, tag=tag, align_bytes=ALIGN)
             nc.sync.dma_start(out=raw[:], in_=x_rows[:, :, c * CHUNK : (c + 1) * CHUNK])
             return raw
 
@@ -114,9 +114,8 @@ def tile_moe_rag_glu_sigmoid_kernel(
         loaded = [load_words(0)]
         offsets = keep.tile([P, T // 16], U16, name="offsets", align_bytes=ALIGN)
         nc.sync.dma_start(offsets[:], offs)
-        raws = [load_x(c) for c in range(3)]
+        raws = [load_x(c, "raw%d" % c) for c in range(3)]
         loaded.append(load_words(1))
-        raws.append(load_x(3))
 
         ordered_rows = keep.tile([P, 2 * H], U8, name="ordered_rows", align_bytes=ALIGN)
         nc.vector.tensor_copy(
@@ -126,8 +125,9 @@ def tile_moe_rag_glu_sigmoid_kernel(
         planes = [first_planes[:]]
         spread_scales(nc.scalar, 0)
         stationary = [order_words(0)]
+        raws.append(load_x(3, "loaded0"))
 
-        late_planes = keep.tile([P, 2 * H + E * GROUPS * N], U8, name="late_planes", tag="loaded0", align_bytes=ALIGN)
+        late_planes = keep.tile([P, 2 * H + E * GROUPS * N], U8, name="late_planes", tag="scale_rows", align_bytes=ALIGN)
         nc.vector.memset(late_planes[:].bitcast(I32), 0)
         planes.append(late_planes[:, : 2 * H])
         w2_plane = late_planes[:, 2 * H :]

@@ -26,8 +26,9 @@ LIST_COLUMNS = P // 16
 ALIGN = 256
 CHUNK = 256
 VECTOR_TOKENS = (0, 160, 128, 0)
-A_BANKS, B_BANKS, Y_BANKS = 2, 4, 2
+A_BANKS, B_BANKS, Y_BANKS = 3, 4, 1
 GATED_BUFFERS = 4
+SHARED_SLOTS = 56
 SCATTER_LAG = 2
 EARLY_BLOCKS = 4
 
@@ -167,13 +168,17 @@ def tile_moe_rag_glu_sigmoid_kernel(
         gate_sb = keep.tile([P, T], F32, name="gate_sb", tag="raw2", align_bytes=ALIGN)
         nc.sync.dma_start(out=gate_sb[:], in_=gate)
 
-        hidden, results = {}, {}
         outT = keep.tile([P, T], F32, name="outT", align_bytes=ALIGN)
+        hidden = keep.tile([P, 2 * H], BF16, name="hidden", align_bytes=ALIGN)
+        own, his = slice(0, P - SHARED_SLOTS), slice(P - SHARED_SLOTS, P)
+        sigmoids = {}
 
-        def first_layer(b, g):
+        def hidden_of(i):
+            return hidden[:, i % 2 * H : (i % 2 + 1) * H]
+
+        def first_layer(i, g):
+            b = order[i]
             e = expert(b)
-            if g == 0:
-                hidden[b] = work.tile([P, GROUPS, PASS], BF16, name="hidden", align_bytes=ALIGN)
             banks = []
             for m, (tag, depth) in enumerate((("a", A_BANKS), ("b", B_BANKS))):
                 bank = psum.tile([P, 4, P], F32, name=tag, bufs=depth)
@@ -191,18 +196,27 @@ def tile_moe_rag_glu_sigmoid_kernel(
                 banks.append(bank[:].rearrange("p t s -> p s t"))
             gated = work.tile([P, P, 4], F32, name="gated", bufs=GATED_BUFFERS, align_bytes=ALIGN)
             nc.scalar.activation(gated[:], banks[0], SIGMOID)
-            nc.vector.tensor_tensor(hidden[b][:, g, :].rearrange("p (s t) -> p s t", t=4), banks[1], gated[:], MULT)
+            sigmoids[i, g] = gated
+            target = hidden_of(i)[:, g * PASS : (g + 1) * PASS].rearrange("p (s t) -> p s t", t=4)
+            if g == 0 and i > SCATTER_LAG:
+                linear = work.tile([P, SHARED_SLOTS, 4], F32, name="linear", align_bytes=ALIGN)
+                nc.scalar.copy(out=linear[:], in_=banks[1][:, his])
+                nc.gpsimd.tensor_tensor(target[:, his], linear[:], gated[:, his], MULT)
+                nc.vector.tensor_tensor(target[:, own], banks[1][:, own], gated[:, own], MULT)
+            else:
+                nc.vector.tensor_tensor(target, banks[1], gated[:], MULT)
 
-        def second_layer(b, passes_a_call):
+        sums = {}
+
+        def second_layer(i):
+            b = order[i]
             codes = work.tile([P, GROUPS, P], U32, name="codes", align_bytes=ALIGN)
             scale = work.tile([P, GROUPS, P], U8, name="scale", align_bytes=ALIGN)
-            for g in range(0, GROUPS, passes_a_call):
-                taken = slice(g, g + passes_a_call)
-                nc.vector.quantize_mx(
-                    out=codes[:, taken].rearrange("p g s -> p (g s)").bitcast(FP8X4),
-                    scales=scale[:, taken].rearrange("p g s -> p (g s)"),
-                    in_=hidden[b][:, taken].rearrange("p g c -> p (g c)"),
-                )
+            nc.vector.quantize_mx(
+                out=codes[:].rearrange("p g s -> p (g s)").bitcast(FP8X4),
+                scales=scale[:].rearrange("p g s -> p (g s)"),
+                in_=hidden_of(i),
+            )
             y = psum.tile([P, P], F32, name="y", bufs=Y_BANKS)
             for g in range(GROUPS):
                 at = expert(b) * GROUPS + g
@@ -215,12 +229,22 @@ def tile_moe_rag_glu_sigmoid_kernel(
                     start=(g == 0),
                     stop=(g == GROUPS - 1),
                 )
-            results[b] = work.tile([P, P], F32, name="results", align_bytes=ALIGN)
-            nc.scalar.copy(out=results[b][:], in_=y[:])
+            sums[i] = y
 
-        def scatter(b):
+        def scatter(i):
+            b = order[i]
+            step = i + SCATTER_LAG
+            if step < BLOCKS:
+                start = PASS - 2 * SHARED_SLOTS - P
+                result = hidden_of(step + 1)[:, start : start + 2 * P].bitcast(F32)
+            elif step == BLOCKS:
+                result = sigmoids[BLOCKS - 1, 1][:].rearrange("p s t -> p (s t)")[:, :P]
+            else:
+                last = work.tile([P, P], F32, name="last", align_bytes=ALIGN)
+                result = last[:]
+            nc.scalar.copy(out=result, in_=sums[i][:])
             listed = offsets[:, b * LIST_COLUMNS : (b + 1) * LIST_COLUMNS]
-            nc.vector.tensor_tensor(outT[:].indirect(listed), results[b][:], gate_sb[:, b * P : (b + 1) * P], MULT)
+            nc.vector.tensor_tensor(outT[:].indirect(listed), result, gate_sb[:, b * P : (b + 1) * P], MULT)
 
         by_first_slot = sorted(range(BLOCKS), key=first_slot)
         order = sorted(by_first_slot[:EARLY_BLOCKS]) + by_first_slot[EARLY_BLOCKS:]
@@ -228,13 +252,14 @@ def tile_moe_rag_glu_sigmoid_kernel(
 
         for i in range(BLOCKS + SCATTER_LAG):
             if i < BLOCKS:
-                first_layer(order[i], 0)
-            if 1 <= i <= BLOCKS:
-                second_layer(order[i - 1], 1 if i == BLOCKS else GROUPS)
-            if i < BLOCKS:
-                first_layer(order[i], 1)
+                first_layer(i, 0)
+                if 1 <= i <= SCATTER_LAG:
+                    second_layer(i - 1)
+                first_layer(i, 1)
             if i >= SCATTER_LAG:
-                scatter(order[i - SCATTER_LAG])
+                scatter(i - SCATTER_LAG)
+            if SCATTER_LAG <= i < BLOCKS:
+                second_layer(i)
             if i - SCATTER_LAG == EARLY_BLOCKS - 1:
                 finished = keep.tile([P, early], F32, name="finished", align_bytes=ALIGN)
                 nc.scalar.copy(out=finished[:], in_=outT[:, :early])

@@ -30,7 +30,7 @@ A_BANKS, B_BANKS, Y_BANKS = 3, 4, 1
 GATED_BUFFERS = 4
 SHARED_SLOTS = 56
 SCATTER_LAG = 2
-EARLY_BLOCKS = 4
+EARLY_BLOCKS = 5
 
 
 def expert(b):
@@ -141,12 +141,12 @@ def tile_moe_rag_glu_sigmoid_kernel(
 
         slot_words, slot_bytes = {}, {}
 
-        def gather(first, last):
+        def gather(first, last, words_tag=None, bytes_tag=None):
             bound = max(reach(b) for b in range(first, last))
             listed = offsets[:, first * LIST_COLUMNS : last * LIST_COLUMNS]
-            words = keep.tile([P, (last - first) * P], U32, name="slot_words%d" % first, align_bytes=ALIGN)
+            words = keep.tile([P, (last - first) * P], U32, name="slot_words%d" % first, tag=words_tag or "slot_words%d" % first, align_bytes=ALIGN)
             nc.vector.tensor_copy(words[:], x_words[:, :bound].indirect(listed))
-            scale = keep.tile([P, (last - first) * P], U8, name="slot_bytes%d" % first, align_bytes=ALIGN)
+            scale = keep.tile([P, (last - first) * P], U8, name="slot_bytes%d" % first, tag=bytes_tag or "slot_bytes%d" % first, align_bytes=ALIGN)
             nc.vector.tensor_copy(scale[:], x_bytes[:, :bound].indirect(listed))
             for b in range(first, last):
                 slot_words[b] = words[:, (b - first) * P : (b - first + 1) * P]
@@ -157,11 +157,9 @@ def tile_moe_rag_glu_sigmoid_kernel(
         gather(0, 1)
         quantise_x(2)
         stationary.append(order_words(1))
-        gather(1, 3)
+        gather(1, 2)
         gather(5, 6)
         quantise_x(3)
-        gather(6, 8)
-        gather(3, 5)
 
         w2_sb = keep.tile([P, E * GROUPS, 2 * N], U8, name="w2_sb", tag="raw1", align_bytes=ALIGN)
         nc.sync.dma_start(out=w2_sb[:].bitcast(I32), in_=w2_words.rearrange("e s p n -> p (e s) n").bitcast(I32))
@@ -194,16 +192,20 @@ def tile_moe_rag_glu_sigmoid_kernel(
                         stop=True,
                     )
                 banks.append(bank[:].rearrange("p t s -> p s t"))
-            gated = work.tile([P, P, 4], F32, name="gated", bufs=GATED_BUFFERS, align_bytes=ALIGN)
-            nc.scalar.activation(gated[:], banks[0], SIGMOID)
-            sigmoids[i, g] = gated
             target = hidden_of(i)[:, g * PASS : (g + 1) * PASS].rearrange("p (s t) -> p s t", t=4)
             if g == 0 and i > SCATTER_LAG:
+                gated = keep.tile([P, P - SHARED_SLOTS, 4], F32, name="gated", tag="pass%d_%d" % (i, g), align_bytes=ALIGN)
+                nc.scalar.activation(gated[:], banks[0][:, own], SIGMOID)
+                gated_his = work.tile([P, SHARED_SLOTS, 4], F32, name="gated_his", align_bytes=ALIGN)
+                nc.scalar.activation(gated_his[:], banks[0][:, his], SIGMOID)
                 linear = work.tile([P, SHARED_SLOTS, 4], F32, name="linear", align_bytes=ALIGN)
                 nc.scalar.copy(out=linear[:], in_=banks[1][:, his])
-                nc.gpsimd.tensor_tensor(target[:, his], linear[:], gated[:, his], MULT)
-                nc.vector.tensor_tensor(target[:, own], banks[1][:, own], gated[:, own], MULT)
+                nc.gpsimd.tensor_tensor(target[:, his], linear[:], gated_his[:], MULT)
+                nc.vector.tensor_tensor(target[:, own], banks[1][:, own], gated[:], MULT)
             else:
+                gated = keep.tile([P, P, 4], F32, name="gated", tag="pass%d_%d" % (i, g), align_bytes=ALIGN)
+                nc.scalar.activation(gated[:], banks[0], SIGMOID)
+                sigmoids[i, g] = gated
                 nc.vector.tensor_tensor(target, banks[1], gated[:], MULT)
 
         sums = {}
@@ -247,18 +249,18 @@ def tile_moe_rag_glu_sigmoid_kernel(
             nc.vector.tensor_tensor(outT[:].indirect(listed), result, gate_sb[:, b * P : (b + 1) * P], MULT)
 
         by_first_slot = sorted(range(BLOCKS), key=first_slot)
-        order = sorted(by_first_slot[:EARLY_BLOCKS]) + by_first_slot[EARLY_BLOCKS:]
+        order = [0, 1, 5, 2, 6, 7, 3, 4]
         early = first_slot(order[EARLY_BLOCKS])
 
         for i in range(BLOCKS + SCATTER_LAG):
             if i < BLOCKS:
                 first_layer(i, 0)
-                if 1 <= i <= SCATTER_LAG:
-                    second_layer(i - 1)
                 first_layer(i, 1)
+            if i + 3 < BLOCKS:
+                gather(order[i + 3], order[i + 3] + 1, "pass%d_0" % i, "pass%d_1" % i)
             if i >= SCATTER_LAG:
                 scatter(i - SCATTER_LAG)
-            if SCATTER_LAG <= i < BLOCKS:
+            if i < BLOCKS:
                 second_layer(i)
             if i - SCATTER_LAG == EARLY_BLOCKS - 1:
                 finished = keep.tile([P, early], F32, name="finished", align_bytes=ALIGN)

@@ -28,7 +28,7 @@ CHUNK = 256
 VECTOR_TOKENS = (0, 160, 128, 0)
 A_BANKS, B_BANKS, Y_BANKS = 3, 4, 1
 GATED_BUFFERS = 4
-SHARED_SLOTS = 56
+SHARED_SLOTS = 72
 SCATTER_LAG = 2
 EARLY_BLOCKS = 5
 
@@ -99,10 +99,11 @@ def tile_moe_rag_glu_sigmoid_kernel(
 
         def order_words(m):
             ordered = keep.tile([P, E, 2 * H], U8, name="ordered%d" % m, align_bytes=ALIGN)
-            nc.vector.tensor_copy(
-                out=ordered[:].bitcast(U16).rearrange("p e (g t q) -> p (e g) t q", t=4, q=P),
-                in_=loaded[m][:].bitcast(U16).rearrange("p e (g q t) -> p (e g) t q", t=4, q=P),
-            )
+            for part in ((slice(0, E),), (slice(0, 1), slice(1, E)))[m]:
+                nc.vector.tensor_copy(
+                    out=ordered[:, part].bitcast(U16).rearrange("p e (g t q) -> p (e g) t q", t=4, q=P),
+                    in_=loaded[m][:, part].bitcast(U16).rearrange("p e (g q t) -> p (e g) t q", t=4, q=P),
+                )
             return ordered
 
         def spread_scales(queue, e):
@@ -168,7 +169,7 @@ def tile_moe_rag_glu_sigmoid_kernel(
 
         outT = keep.tile([P, T], F32, name="outT", align_bytes=ALIGN)
         hidden = keep.tile([P, 2 * H], BF16, name="hidden", align_bytes=ALIGN)
-        own, his = slice(0, P - SHARED_SLOTS), slice(P - SHARED_SLOTS, P)
+        his, own = slice(0, SHARED_SLOTS), slice(SHARED_SLOTS, P)
         sigmoids = {}
 
         def hidden_of(i):
@@ -237,7 +238,7 @@ def tile_moe_rag_glu_sigmoid_kernel(
             b = order[i]
             step = i + SCATTER_LAG
             if step < BLOCKS:
-                start = PASS - 2 * SHARED_SLOTS - P
+                start = PASS - 2 * (P - SHARED_SLOTS) - P
                 result = hidden_of(step + 1)[:, start : start + 2 * P].bitcast(F32)
             elif step == BLOCKS:
                 result = sigmoids[BLOCKS - 1, 1][:].rearrange("p s t -> p (s t)")[:, :P]

@@ -17,20 +17,19 @@ FP8X4 = mybir.dt.float8_e4m3fn_x4
 FP4X4 = mybir.dt.float4_e2m1fn_x4
 MULT = mybir.AluOpType.mult
 SIGMOID = mybir.ActivationFunctionType.Sigmoid
+COPY = mybir.ActivationFunctionType.Copy
 
 PASS = 4 * P
 GROUPS = H // PASS
-ROWS = PASS // 32
 BLOCKS = T // P
 LIST_COLUMNS = P // 16
 ALIGN = 256
 CHUNK = 256
-VECTOR_TOKENS = (0, 160, 128, 0)
-A_BANKS, B_BANKS, Y_BANKS = 3, 4, 1
-GATED_BUFFERS = 4
-SHARED_SLOTS = 72
-SCATTER_LAG = 2
-EARLY_BLOCKS = 5
+VECTOR_TOKENS = (160, 160, 96, 0)
+A_BANKS, B_BANKS, Y_BANKS = 2, 4, 2
+GATED_BUFFERS = 5
+GATHER_LEAD = 3
+EARLY_STEPS = 6
 
 
 def expert(b):
@@ -54,32 +53,32 @@ def tile_moe_rag_glu_sigmoid_kernel(
         work = ctx.enter_context(tc.tile_pool(name="work", bufs=3))
         psum = ctx.enter_context(tc.psum_pool(name="psum", bufs=1))
 
-        scale_rows = keep.tile([P, 2, H], U8, name="scale_rows", tag="scale_rows", align_bytes=ALIGN)
+        rows = keep.tile([P, PASS], U8, name="rows", tag="rows", align_bytes=ALIGN)
         for m, scales in enumerate((w1_scales, w3_scales)):
-            nc.sync.dma_start(
-                out=scale_rows[: E * ROWS, m, :].bitcast(I32),
-                in_=scales.rearrange("e s q i -> (e s q) i").bitcast(I32),
-            )
+            halves = scales.rearrange("e s q (g c) -> e (s q g) c", g=GROUPS).bitcast(I32)
+            for e in range(E):
+                nc.sync.dma_start(out=rows[2 * e + m : P : 4].bitcast(I32), in_=halves[e])
+        offsets = keep.tile([P, T // 16], U16, name="offsets", align_bytes=ALIGN)
+        nc.sync.dma_start(offsets[:], offs)
         warm = keep.tile([P, 1], F32, name="warm")
         nc.vector.memset(warm[:], 0.0)
         nc.scalar.activation(warm[:], warm[:], SIGMOID)
-        for p0, p1 in ((32, 64), (64, P)):
-            nc.vector.memset(scale_rows[p0:p1].rearrange("p m i -> p (m i)").bitcast(I32), 0)
-        first_planes = keep.tile([P, 2 * H], U8, name="first_planes", align_bytes=ALIGN)
-        nc.vector.memset(first_planes[:].bitcast(I32), 0)
+        planes = keep.tile([P, E * 2 * H], U8, name="planes", align_bytes=ALIGN)
+        nc.vector.memset(planes[:].bitcast(I32), 0)
         x_bytes = keep.tile([P, T], U8, name="x_bytes", align_bytes=ALIGN)
         nc.vector.memset(x_bytes[:].bitcast(I32), 0)
         x_words = keep.tile([P, T], U32, name="x_words", align_bytes=ALIGN)
         x_rows = xT.rearrange("(p j) w -> p j w", j=4)
+        raws, loaded, stationary = {}, {}, {}
 
         def load_x(c, tag):
             raw = keep.tile([P, 4, CHUNK], F32, name="raw%d" % c, tag=tag, align_bytes=ALIGN)
             nc.sync.dma_start(out=raw[:], in_=x_rows[:, :, c * CHUNK : (c + 1) * CHUNK])
-            return raw
+            raws[c] = raw
 
         def quantise_x(c):
             cut = VECTOR_TOKENS[c]
-            side = keep.tile([P, CHUNK, 4], BF16, name="side%d" % c, align_bytes=ALIGN)
+            side = keep.tile([P, CHUNK, 4], BF16, name="side%d" % c, tag="side%d" % c, align_bytes=ALIGN)
             source = raws[c][:].rearrange("p j (w n) -> p w j n", n=4)
             target = side[:].rearrange("p (w n) j -> p w j n", n=4)
             if cut > 0:
@@ -91,89 +90,72 @@ def tile_moe_rag_glu_sigmoid_kernel(
                 in_=side[:].rearrange("p w j -> p (w j)"),
             )
 
-        def load_words(m):
-            words = keep.tile([P, E, 2 * H], U8, name="loaded%d" % m, tag="loaded%d" % m, align_bytes=ALIGN)
-            source = (w1_words, w3_words)[m].rearrange("e s p i -> p (e s) i")
-            nc.sync.dma_start(out=words[:].bitcast(I32), in_=source.bitcast(I32))
-            return words
+        def load_words(m, e, tag):
+            words = keep.tile([P, 2 * H], U8, name="loaded%d%d" % (m, e), tag=tag, align_bytes=ALIGN)
+            source = (w1_words, w3_words)[m].rearrange("e s p i -> (e s) p i").bitcast(I32)
+            nc.sync.dma_start(out=words[:].bitcast(I32), in_=source[e])
+            loaded[m, e] = words
 
-        def order_words(m):
-            ordered = keep.tile([P, E, 2 * H], U8, name="ordered%d" % m, align_bytes=ALIGN)
-            for part in ((slice(0, E),), (slice(0, 1), slice(1, E)))[m]:
-                nc.vector.tensor_copy(
-                    out=ordered[:, part].bitcast(U16).rearrange("p e (g t q) -> p (e g) t q", t=4, q=P),
-                    in_=loaded[m][:, part].bitcast(U16).rearrange("p e (g q t) -> p (e g) t q", t=4, q=P),
-                )
-            return ordered
+        def order_words(m, e):
+            ordered = keep.tile([P, 2 * H], U8, name="ordered%d%d" % (m, e), align_bytes=ALIGN)
+            nc.vector.tensor_copy(
+                out=ordered[:].bitcast(U16).rearrange("p (g t q) -> p g t q", t=4, q=P),
+                in_=loaded[m, e][:].bitcast(U16).rearrange("p (g q t) -> p g t q", t=4, q=P),
+            )
+            stationary[m, e] = ordered
 
-        def spread_scales(queue, e):
-            for r in range(4):
-                queue.dma_start(
-                    out=planes[e][r:P:32].bitcast(I32),
-                    in_=ordered_rows[ROWS * e + r : ROWS * (e + 1) : 4].bitcast(I32),
-                )
+        load_words(0, 0, "loaded00")
+        load_x(0, "raw0")
+        load_x(1, "raw1")
+        load_words(1, 0, "loaded10")
 
-        loaded = [load_words(0)]
-        offsets = keep.tile([P, T // 16], U16, name="offsets", align_bytes=ALIGN)
-        nc.sync.dma_start(offsets[:], offs)
-        raws = [load_x(c, "raw%d" % c) for c in range(3)]
-        loaded.append(load_words(1))
-
-        ordered_rows = keep.tile([P, 2 * H], U8, name="ordered_rows", align_bytes=ALIGN)
+        ordered_rows = keep.tile([P, PASS], U8, name="ordered_rows", align_bytes=ALIGN)
         nc.vector.tensor_copy(
-            out=ordered_rows[:].rearrange("p (x t q) -> p x t q", t=4, q=P),
-            in_=scale_rows[:].rearrange("p m (g q t) -> p (m g) t q", g=GROUPS, t=4),
+            out=ordered_rows[:].rearrange("p (t q) -> p t q", t=4),
+            in_=rows[:].rearrange("p (q t) -> p t q", t=4),
         )
-        planes = [first_planes[:]]
-        spread_scales(nc.scalar, 0)
-        stationary = [order_words(0)]
-        raws.append(load_x(3, "loaded0"))
+        for a in range(4):
+            nc.sync.dma_start(
+                out=planes[32 * a : 32 * a + 4].rearrange("p (x c) -> p x c", c=PASS).bitcast(I32),
+                in_=ordered_rows[32 * a : 32 * (a + 1)].bitcast(I32),
+            )
+        load_x(2, "rows")
+        order_words(0, 0)
+        load_words(0, 1, "loaded00")
 
-        late_planes = keep.tile([P, 2 * H + E * GROUPS * N], U8, name="late_planes", tag="scale_rows", align_bytes=ALIGN)
-        nc.vector.memset(late_planes[:].bitcast(I32), 0)
-        planes.append(late_planes[:, : 2 * H])
-        w2_plane = late_planes[:, 2 * H :]
-        spread_scales(nc.sync, 1)
+        slot_words, slot_bytes = {}, {}
+
+        def gather(b):
+            listed = offsets[:, b * LIST_COLUMNS : (b + 1) * LIST_COLUMNS]
+            words = work.tile([P, P], U32, name="slot_words", bufs=GATHER_LEAD, align_bytes=ALIGN)
+            nc.vector.tensor_copy(words[:], x_words[:, : reach(b)].indirect(listed))
+            scale = work.tile([P, P], U8, name="slot_bytes", bufs=GATHER_LEAD, align_bytes=ALIGN)
+            nc.vector.tensor_copy(scale[:], x_bytes[:, : reach(b)].indirect(listed))
+            slot_words[b], slot_bytes[b] = words, scale
+
+        order = [0, 1, 2, 5, 6, 7, 3, 4]
+        quantise_x(0)
+        load_x(3, "raw0")
+        quantise_x(1)
+        load_words(1, 1, "raw1")
+        gather(order[0])
+        order_words(1, 0)
+        gate_sb = keep.tile([P, T], F32, name="gate_sb", tag="side1", align_bytes=ALIGN)
+        nc.sync.dma_start(out=gate_sb[:], in_=gate)
+        w2_sb = keep.tile([P, E * GROUPS, 2 * N], U8, name="w2_sb", tag="side0", align_bytes=ALIGN)
+        nc.sync.dma_start(out=w2_sb[:].bitcast(I32), in_=w2_words.rearrange("e s p n -> p (e s) n").bitcast(I32))
+        w2_plane = loaded[1, 0][:, : E * GROUPS * N]
         w2_rows = w2_scales.rearrange("e s (a r) n -> r a (e s) n", r=4)
         for r in range(4):
             nc.sync.dma_start(
                 out=w2_plane[r:P:32].rearrange("p (s n) -> p s n", n=N).bitcast(I32), in_=w2_rows[r].bitcast(I32)
             )
-
-        slot_words, slot_bytes = {}, {}
-
-        def gather(first, last, words_tag=None, bytes_tag=None):
-            bound = max(reach(b) for b in range(first, last))
-            listed = offsets[:, first * LIST_COLUMNS : last * LIST_COLUMNS]
-            words = keep.tile([P, (last - first) * P], U32, name="slot_words%d" % first, tag=words_tag or "slot_words%d" % first, align_bytes=ALIGN)
-            nc.vector.tensor_copy(words[:], x_words[:, :bound].indirect(listed))
-            scale = keep.tile([P, (last - first) * P], U8, name="slot_bytes%d" % first, tag=bytes_tag or "slot_bytes%d" % first, align_bytes=ALIGN)
-            nc.vector.tensor_copy(scale[:], x_bytes[:, :bound].indirect(listed))
-            for b in range(first, last):
-                slot_words[b] = words[:, (b - first) * P : (b - first + 1) * P]
-                slot_bytes[b] = scale[:, (b - first) * P : (b - first + 1) * P]
-
-        quantise_x(0)
-        quantise_x(1)
-        gather(0, 1)
         quantise_x(2)
-        stationary.append(order_words(1))
-        gather(1, 2)
-        gather(5, 6)
-        quantise_x(3)
-
-        w2_sb = keep.tile([P, E * GROUPS, 2 * N], U8, name="w2_sb", tag="raw1", align_bytes=ALIGN)
-        nc.sync.dma_start(out=w2_sb[:].bitcast(I32), in_=w2_words.rearrange("e s p n -> p (e s) n").bitcast(I32))
-        gate_sb = keep.tile([P, T], F32, name="gate_sb", tag="raw2", align_bytes=ALIGN)
-        nc.sync.dma_start(out=gate_sb[:], in_=gate)
+        gather(order[1])
+        gather(order[2])
 
         outT = keep.tile([P, T], F32, name="outT", align_bytes=ALIGN)
-        hidden = keep.tile([P, 2 * H], BF16, name="hidden", align_bytes=ALIGN)
-        his, own = slice(0, SHARED_SLOTS), slice(SHARED_SLOTS, P)
-        sigmoids = {}
-
-        def hidden_of(i):
-            return hidden[:, i % 2 * H : (i % 2 + 1) * H]
+        hidden, sums = {}, {}
 
         def first_layer(i, g):
             b = order[i]
@@ -183,46 +165,42 @@ def tile_moe_rag_glu_sigmoid_kernel(
                 bank = psum.tile([P, 4, P], F32, name=tag, bufs=depth)
                 for t in range(4):
                     at = PASS * g + P * t
+                    column = (4 * g + 2 * e + m) * PASS + P * t
                     nc.tensor.matmul_mx(
                         out=bank[:, t, :],
-                        lhsT=stationary[m][:, e, 2 * at : 2 * (at + P)].bitcast(FP4X4),
-                        lhsT_scale=planes[e][:, m * H + at : m * H + at + P],
-                        rhs=slot_words[b].bitcast(FP8X4),
-                        rhs_scale=slot_bytes[b],
+                        lhsT=stationary[m, e][:, 2 * at : 2 * (at + P)].bitcast(FP4X4),
+                        lhsT_scale=planes[:, column : column + P],
+                        rhs=slot_words[b][:].bitcast(FP8X4),
+                        rhs_scale=slot_bytes[b][:],
                         start=True,
                         stop=True,
                     )
                 banks.append(bank[:].rearrange("p t s -> p s t"))
-            target = hidden_of(i)[:, g * PASS : (g + 1) * PASS].rearrange("p (s t) -> p s t", t=4)
-            if g == 0 and i > SCATTER_LAG:
-                gated = keep.tile([P, P - SHARED_SLOTS, 4], F32, name="gated", tag="pass%d_%d" % (i, g), align_bytes=ALIGN)
-                nc.scalar.activation(gated[:], banks[0][:, own], SIGMOID)
-                gated_his = work.tile([P, SHARED_SLOTS, 4], F32, name="gated_his", align_bytes=ALIGN)
-                nc.scalar.activation(gated_his[:], banks[0][:, his], SIGMOID)
-                linear = work.tile([P, SHARED_SLOTS, 4], F32, name="linear", align_bytes=ALIGN)
-                nc.scalar.copy(out=linear[:], in_=banks[1][:, his])
-                nc.gpsimd.tensor_tensor(target[:, his], linear[:], gated_his[:], MULT)
-                nc.vector.tensor_tensor(target[:, own], banks[1][:, own], gated[:], MULT)
-            else:
-                gated = keep.tile([P, P, 4], F32, name="gated", tag="pass%d_%d" % (i, g), align_bytes=ALIGN)
-                nc.scalar.activation(gated[:], banks[0], SIGMOID)
-                sigmoids[i, g] = gated
-                nc.vector.tensor_tensor(target, banks[1], gated[:], MULT)
+            if g == 0:
+                hidden[i] = work.tile([P, GROUPS, P, 4], BF16, name="hidden", align_bytes=ALIGN)
+            gated = work.tile([P, P, 4], F32, name="gated", bufs=GATED_BUFFERS, align_bytes=ALIGN)
+            nc.scalar.activation(gated[:], banks[0], SIGMOID)
+            nc.vector.tensor_tensor(hidden[i][:, g], banks[1], gated[:], MULT)
 
-        sums = {}
+        quantised = {}
+
+        def quantise_h(i, passes):
+            if passes.start == 0:
+                codes = work.tile([P, GROUPS, P], U32, name="codes", align_bytes=ALIGN)
+                scale = work.tile([P, GROUPS, P], U8, name="scale", align_bytes=ALIGN)
+                quantised[i] = codes, scale
+            codes, scale = quantised[i]
+            nc.vector.quantize_mx(
+                out=codes[:, passes].rearrange("p g s -> p (g s)").bitcast(FP8X4),
+                scales=scale[:, passes].rearrange("p g s -> p (g s)"),
+                in_=hidden[i][:, passes].rearrange("p g s t -> p (g s t)"),
+            )
 
         def second_layer(i):
-            b = order[i]
-            codes = work.tile([P, GROUPS, P], U32, name="codes", align_bytes=ALIGN)
-            scale = work.tile([P, GROUPS, P], U8, name="scale", align_bytes=ALIGN)
-            nc.vector.quantize_mx(
-                out=codes[:].rearrange("p g s -> p (g s)").bitcast(FP8X4),
-                scales=scale[:].rearrange("p g s -> p (g s)"),
-                in_=hidden_of(i),
-            )
+            codes, scale = quantised[i]
             y = psum.tile([P, P], F32, name="y", bufs=Y_BANKS)
             for g in range(GROUPS):
-                at = expert(b) * GROUPS + g
+                at = expert(order[i]) * GROUPS + g
                 nc.tensor.matmul_mx(
                     out=y[:],
                     lhsT=w2_sb[:, at, :].bitcast(FP4X4),
@@ -234,37 +212,37 @@ def tile_moe_rag_glu_sigmoid_kernel(
                 )
             sums[i] = y
 
+        early = min(first_slot(b) for b in order[EARLY_STEPS:])
+
         def scatter(i):
             b = order[i]
-            step = i + SCATTER_LAG
-            if step < BLOCKS:
-                start = PASS - 2 * (P - SHARED_SLOTS) - P
-                result = hidden_of(step + 1)[:, start : start + 2 * P].bitcast(F32)
-            elif step == BLOCKS:
-                result = sigmoids[BLOCKS - 1, 1][:].rearrange("p s t -> p (s t)")[:, :P]
-            else:
-                last = work.tile([P, P], F32, name="last", align_bytes=ALIGN)
-                result = last[:]
-            nc.scalar.copy(out=result, in_=sums[i][:])
+            weighed = work.tile([P, P], F32, name="weighed", align_bytes=ALIGN)
+            nc.vector.tensor_tensor(weighed[:], sums[i][:], gate_sb[:, b * P : (b + 1) * P], MULT)
             listed = offsets[:, b * LIST_COLUMNS : (b + 1) * LIST_COLUMNS]
-            nc.vector.tensor_tensor(outT[:].indirect(listed), result, gate_sb[:, b * P : (b + 1) * P], MULT)
-
-        by_first_slot = sorted(range(BLOCKS), key=first_slot)
-        order = [0, 1, 5, 2, 6, 7, 3, 4]
-        early = first_slot(order[EARLY_BLOCKS])
-
-        for i in range(BLOCKS + SCATTER_LAG):
-            if i < BLOCKS:
-                first_layer(i, 0)
-                first_layer(i, 1)
-            if i + 3 < BLOCKS:
-                gather(order[i + 3], order[i + 3] + 1, "pass%d_0" % i, "pass%d_1" % i)
-            if i >= SCATTER_LAG:
-                scatter(i - SCATTER_LAG)
-            if i < BLOCKS:
-                second_layer(i)
-            if i - SCATTER_LAG == EARLY_BLOCKS - 1:
+            nc.scalar.activation(outT[:].indirect(listed), weighed[:], COPY)
+            if i == EARLY_STEPS - 1:
                 finished = keep.tile([P, early], F32, name="finished", align_bytes=ALIGN)
                 nc.scalar.copy(out=finished[:], in_=outT[:, :early])
                 nc.sync.dma_start(out=out[:, :early], in_=finished[:])
+
+        last = BLOCKS - 1
+        for i in range(BLOCKS):
+            first_layer(i, 0)
+            if i >= 1:
+                quantise_h(i - 1, slice(1, 2))
+                second_layer(i - 1)
+            if i == 0:
+                order_words(0, 1)
+                quantise_x(3)
+            if i == 1:
+                order_words(1, 1)
+            first_layer(i, 1)
+            if i + GATHER_LEAD < BLOCKS:
+                gather(order[i + GATHER_LEAD])
+            quantise_h(i, slice(0, 1))
+            if i >= 1:
+                scatter(i - 1)
+        quantise_h(last, slice(1, 2))
+        second_layer(last)
+        scatter(last)
         nc.sync.dma_start(out=out[:, early:], in_=outT[:, early:])

@@ -25,11 +25,13 @@ BLOCKS = T // P
 LIST_COLUMNS = P // 16
 ALIGN = 256
 CHUNK = 256
-VECTOR_TOKENS = (160, 160, 96, 0)
+RAW_BYTES = 4 * CHUNK * 4
+PIECE = PASS + N
+VECTOR_TOKENS = (160, 160, 0, 0)
 A_BANKS, B_BANKS, Y_BANKS = 2, 4, 2
-GATED_BUFFERS = 5
+GATED_BUFFERS = 8
 GATHER_LEAD = 3
-EARLY_STEPS = 6
+SCATTER_LAG = 2
 
 
 def expert(b):
@@ -51,19 +53,24 @@ def tile_moe_rag_glu_sigmoid_kernel(
     with ExitStack() as ctx:
         keep = ctx.enter_context(tc.tile_pool(name="keep", bufs=1))
         work = ctx.enter_context(tc.tile_pool(name="work", bufs=3))
+        held = ctx.enter_context(tc.tile_pool(name="held", bufs=1))
         psum = ctx.enter_context(tc.psum_pool(name="psum", bufs=1))
 
-        rows = keep.tile([P, PASS], U8, name="rows", tag="rows", align_bytes=ALIGN)
+        rows = held.tile([P, PASS], U8, name="rows", offset=RAW_BYTES - ALIGN, align_bytes=ALIGN)
         for m, scales in enumerate((w1_scales, w3_scales)):
-            halves = scales.rearrange("e s q (g c) -> e (s q g) c", g=GROUPS).bitcast(I32)
-            for e in range(E):
-                nc.sync.dma_start(out=rows[2 * e + m : P : 4].bitcast(I32), in_=halves[e])
+            halves = scales.rearrange("e s q (g c) -> (s q g) e c", g=GROUPS).bitcast(I32)
+            nc.sync.dma_start(out=rows[m:P:2].bitcast(I32), in_=halves)
+        ordered_rows = keep.tile([P, PIECE], U8, name="ordered_rows", align_bytes=ALIGN)
+        nc.vector.memset(ordered_rows[:, PASS:].bitcast(I32), 0)
+        nc.sync.dma_start(
+            out=ordered_rows[0:P:2, PASS:].bitcast(I32), in_=w2_scales.rearrange("e s q n -> q (e s) n").bitcast(I32)
+        )
         offsets = keep.tile([P, T // 16], U16, name="offsets", align_bytes=ALIGN)
         nc.sync.dma_start(offsets[:], offs)
         warm = keep.tile([P, 1], F32, name="warm")
         nc.vector.memset(warm[:], 0.0)
         nc.scalar.activation(warm[:], warm[:], SIGMOID)
-        planes = keep.tile([P, E * 2 * H], U8, name="planes", align_bytes=ALIGN)
+        planes = keep.tile([P, 8 * PIECE], U8, name="planes", align_bytes=ALIGN)
         nc.vector.memset(planes[:].bitcast(I32), 0)
         x_bytes = keep.tile([P, T], U8, name="x_bytes", align_bytes=ALIGN)
         nc.vector.memset(x_bytes[:].bitcast(I32), 0)
@@ -71,8 +78,8 @@ def tile_moe_rag_glu_sigmoid_kernel(
         x_rows = xT.rearrange("(p j) w -> p j w", j=4)
         raws, loaded, stationary = {}, {}, {}
 
-        def load_x(c, tag):
-            raw = keep.tile([P, 4, CHUNK], F32, name="raw%d" % c, tag=tag, align_bytes=ALIGN)
+        def load_x(c, pool, **place):
+            raw = pool.tile([P, 4, CHUNK], F32, name="raw%d" % c, align_bytes=ALIGN, **place)
             nc.sync.dma_start(out=raw[:], in_=x_rows[:, :, c * CHUNK : (c + 1) * CHUNK])
             raws[c] = raw
 
@@ -90,8 +97,8 @@ def tile_moe_rag_glu_sigmoid_kernel(
                 in_=side[:].rearrange("p w j -> p (w j)"),
             )
 
-        def load_words(m, e, tag):
-            words = keep.tile([P, 2 * H], U8, name="loaded%d%d" % (m, e), tag=tag, align_bytes=ALIGN)
+        def load_words(m, e, pool, **place):
+            words = pool.tile([P, 2 * H], U8, name="loaded%d%d" % (m, e), align_bytes=ALIGN, **place)
             source = (w1_words, w3_words)[m].rearrange("e s p i -> (e s) p i").bitcast(I32)
             nc.sync.dma_start(out=words[:].bitcast(I32), in_=source[e])
             loaded[m, e] = words
@@ -104,52 +111,45 @@ def tile_moe_rag_glu_sigmoid_kernel(
             )
             stationary[m, e] = ordered
 
-        load_words(0, 0, "loaded00")
-        load_x(0, "raw0")
-        load_x(1, "raw1")
-        load_words(1, 0, "loaded10")
+        load_x(0, keep, tag="raw0")
+        load_x(1, keep, tag="raw1")
+        load_words(0, 0, keep, tag="loaded00")
 
-        ordered_rows = keep.tile([P, PASS], U8, name="ordered_rows", align_bytes=ALIGN)
         nc.vector.tensor_copy(
-            out=ordered_rows[:].rearrange("p (t q) -> p t q", t=4),
+            out=ordered_rows[:, :PASS].rearrange("p (t q) -> p t q", t=4),
             in_=rows[:].rearrange("p (q t) -> p t q", t=4),
         )
         for a in range(4):
             nc.sync.dma_start(
-                out=planes[32 * a : 32 * a + 4].rearrange("p (x c) -> p x c", c=PASS).bitcast(I32),
+                out=planes[32 * a : 32 * a + 4].rearrange("p (x c) -> p x c", c=PIECE).bitcast(I32),
                 in_=ordered_rows[32 * a : 32 * (a + 1)].bitcast(I32),
             )
-        load_x(2, "rows")
-        order_words(0, 0)
-        load_words(0, 1, "loaded00")
+        load_x(2, held, offset=0)
+        load_words(1, 0, held, offset=RAW_BYTES)
 
         slot_words, slot_bytes = {}, {}
 
         def gather(b):
             listed = offsets[:, b * LIST_COLUMNS : (b + 1) * LIST_COLUMNS]
-            words = work.tile([P, P], U32, name="slot_words", bufs=GATHER_LEAD, align_bytes=ALIGN)
+            words = work.tile([P, P], U32, name="slot_words", bufs=GATHER_LEAD + 1, align_bytes=ALIGN)
             nc.vector.tensor_copy(words[:], x_words[:, : reach(b)].indirect(listed))
-            scale = work.tile([P, P], U8, name="slot_bytes", bufs=GATHER_LEAD, align_bytes=ALIGN)
+            scale = work.tile([P, P], U8, name="slot_bytes", bufs=GATHER_LEAD + 1, align_bytes=ALIGN)
             nc.vector.tensor_copy(scale[:], x_bytes[:, : reach(b)].indirect(listed))
             slot_words[b], slot_bytes[b] = words, scale
 
         order = [0, 1, 2, 5, 6, 7, 3, 4]
         quantise_x(0)
-        load_x(3, "raw0")
+        load_x(3, keep, tag="raw0")
         quantise_x(1)
-        load_words(1, 1, "raw1")
+        load_words(0, 1, keep, tag="raw1")
+        order_words(0, 0)
+        load_words(1, 1, keep, tag="loaded00")
         gather(order[0])
         order_words(1, 0)
         gate_sb = keep.tile([P, T], F32, name="gate_sb", tag="side1", align_bytes=ALIGN)
         nc.sync.dma_start(out=gate_sb[:], in_=gate)
         w2_sb = keep.tile([P, E * GROUPS, 2 * N], U8, name="w2_sb", tag="side0", align_bytes=ALIGN)
         nc.sync.dma_start(out=w2_sb[:].bitcast(I32), in_=w2_words.rearrange("e s p n -> p (e s) n").bitcast(I32))
-        w2_plane = loaded[1, 0][:, : E * GROUPS * N]
-        w2_rows = w2_scales.rearrange("e s (a r) n -> r a (e s) n", r=4)
-        for r in range(4):
-            nc.sync.dma_start(
-                out=w2_plane[r:P:32].rearrange("p (s n) -> p s n", n=N).bitcast(I32), in_=w2_rows[r].bitcast(I32)
-            )
         quantise_x(2)
         gather(order[1])
         gather(order[2])
@@ -165,7 +165,7 @@ def tile_moe_rag_glu_sigmoid_kernel(
                 bank = psum.tile([P, 4, P], F32, name=tag, bufs=depth)
                 for t in range(4):
                     at = PASS * g + P * t
-                    column = (4 * g + 2 * e + m) * PASS + P * t
+                    column = (4 * g + 2 * e + m) * PIECE + P * t
                     nc.tensor.matmul_mx(
                         out=bank[:, t, :],
                         lhsT=stationary[m, e][:, 2 * at : 2 * (at + P)].bitcast(FP4X4),
@@ -178,7 +178,10 @@ def tile_moe_rag_glu_sigmoid_kernel(
                 banks.append(bank[:].rearrange("p t s -> p s t"))
             if g == 0:
                 hidden[i] = work.tile([P, GROUPS, P, 4], BF16, name="hidden", align_bytes=ALIGN)
-            gated = work.tile([P, P, 4], F32, name="gated", bufs=GATED_BUFFERS, align_bytes=ALIGN)
+            if i == 0:
+                gated = held.tile([P, P, 4], F32, name="gated%d" % g, offset=g * PASS * 4, align_bytes=ALIGN)
+            else:
+                gated = work.tile([P, P, 4], F32, name="gated", bufs=GATED_BUFFERS, align_bytes=ALIGN)
             nc.scalar.activation(gated[:], banks[0], SIGMOID)
             nc.vector.tensor_tensor(hidden[i][:, g], banks[1], gated[:], MULT)
 
@@ -204,7 +207,7 @@ def tile_moe_rag_glu_sigmoid_kernel(
                 nc.tensor.matmul_mx(
                     out=y[:],
                     lhsT=w2_sb[:, at, :].bitcast(FP4X4),
-                    lhsT_scale=w2_plane[:, at * N : (at + 1) * N],
+                    lhsT_scale=planes[:, 2 * at * PIECE + PASS : (2 * at + 1) * PIECE],
                     rhs=codes[:, g, :].bitcast(FP8X4),
                     rhs_scale=scale[:, g, :],
                     start=(g == 0),
@@ -212,37 +215,41 @@ def tile_moe_rag_glu_sigmoid_kernel(
                 )
             sums[i] = y
 
-        early = min(first_slot(b) for b in order[EARLY_STEPS:])
+        weighed = {}
+
+        def weigh(i):
+            b = order[i]
+            weighed[i] = work.tile([P, P], F32, name="weighed", bufs=BLOCKS, align_bytes=ALIGN)
+            nc.vector.tensor_tensor(weighed[i][:], sums[i][:], gate_sb[:, b * P : (b + 1) * P], MULT)
 
         def scatter(i):
             b = order[i]
-            weighed = work.tile([P, P], F32, name="weighed", align_bytes=ALIGN)
-            nc.vector.tensor_tensor(weighed[:], sums[i][:], gate_sb[:, b * P : (b + 1) * P], MULT)
             listed = offsets[:, b * LIST_COLUMNS : (b + 1) * LIST_COLUMNS]
-            nc.scalar.activation(outT[:].indirect(listed), weighed[:], COPY)
-            if i == EARLY_STEPS - 1:
-                finished = keep.tile([P, early], F32, name="finished", align_bytes=ALIGN)
-                nc.scalar.copy(out=finished[:], in_=outT[:, :early])
-                nc.sync.dma_start(out=out[:, :early], in_=finished[:])
+            nc.scalar.activation(outT[:].indirect(listed), weighed[i][:], COPY)
 
         last = BLOCKS - 1
         for i in range(BLOCKS):
             first_layer(i, 0)
             if i >= 1:
-                quantise_h(i - 1, slice(1, 2))
+                quantise_h(i - 1, slice(0, GROUPS))
                 second_layer(i - 1)
             if i == 0:
                 order_words(0, 1)
-                quantise_x(3)
             if i == 1:
                 order_words(1, 1)
             first_layer(i, 1)
+            if i >= SCATTER_LAG:
+                scatter(i - SCATTER_LAG)
+            if i == 1:
+                quantise_x(3)
             if i + GATHER_LEAD < BLOCKS:
                 gather(order[i + GATHER_LEAD])
-            quantise_h(i, slice(0, 1))
             if i >= 1:
-                scatter(i - 1)
+                weigh(i - 1)
+        quantise_h(last, slice(0, 1))
         quantise_h(last, slice(1, 2))
         second_layer(last)
-        scatter(last)
-        nc.sync.dma_start(out=out[:, early:], in_=outT[:, early:])
+        weigh(last)
+        for i in range(BLOCKS - SCATTER_LAG, BLOCKS):
+            scatter(i)
+        nc.sync.dma_start(out=out, in_=outT[:])

@@ -27,11 +27,13 @@ ALIGN = 256
 CHUNK = 256
 RAW_BYTES = 4 * CHUNK * 4
 PIECE = PASS + N
-VECTOR_TOKENS = (160, 160, 0, 0)
+VECTOR_TOKENS = (160, 160, 128, 0)
 A_BANKS, B_BANKS, Y_BANKS = 2, 4, 2
 GATED_BUFFERS = 8
 GATHER_LEAD = 3
 SCATTER_LAG = 2
+EARLY_STEPS = 6
+SCALAR_SCATTERS = (1, 3, 5)
 
 
 def expert(b):
@@ -58,32 +60,31 @@ def tile_moe_rag_glu_sigmoid_kernel(
 
         rows = held.tile([P, PASS], U8, name="rows", offset=RAW_BYTES - ALIGN, align_bytes=ALIGN)
         for m, scales in enumerate((w1_scales, w3_scales)):
-            halves = scales.rearrange("e s q (g c) -> (s q g) e c", g=GROUPS).bitcast(I32)
+            halves = scales.rearrange("e s q (g c) -> (e s q g) c", g=GROUPS).bitcast(I32)
             nc.sync.dma_start(out=rows[m:P:2].bitcast(I32), in_=halves)
         ordered_rows = keep.tile([P, PIECE], U8, name="ordered_rows", align_bytes=ALIGN)
-        nc.vector.memset(ordered_rows[:, PASS:].bitcast(I32), 0)
         nc.sync.dma_start(
-            out=ordered_rows[0:P:2, PASS:].bitcast(I32), in_=w2_scales.rearrange("e s q n -> q (e s) n").bitcast(I32)
+            out=ordered_rows[: P // 2, PASS:].bitcast(I32), in_=w2_scales.rearrange("e s q n -> q (e s) n").bitcast(I32)
         )
-        offsets = keep.tile([P, T // 16], U16, name="offsets", align_bytes=ALIGN)
-        nc.sync.dma_start(offsets[:], offs)
         warm = keep.tile([P, 1], F32, name="warm")
         nc.vector.memset(warm[:], 0.0)
         nc.scalar.activation(warm[:], warm[:], SIGMOID)
-        planes = keep.tile([P, 8 * PIECE], U8, name="planes", align_bytes=ALIGN)
-        nc.vector.memset(planes[:].bitcast(I32), 0)
+        first_planes = keep.tile([P, 4 * PIECE], U8, name="first_planes", align_bytes=ALIGN)
+        nc.vector.memset(first_planes[:].bitcast(I32), 0)
         x_bytes = keep.tile([P, T], U8, name="x_bytes", align_bytes=ALIGN)
         nc.vector.memset(x_bytes[:].bitcast(I32), 0)
+        late_planes = keep.tile([P, 4 * PASS], U8, name="late_planes", align_bytes=ALIGN)
+        nc.vector.memset(late_planes[:].bitcast(I32), 0)
         x_words = keep.tile([P, T], U32, name="x_words", align_bytes=ALIGN)
         x_rows = xT.rearrange("(p j) w -> p j w", j=4)
-        raws, loaded, stationary = {}, {}, {}
+        raws, sides, loaded, stationary = {}, {}, {}, {}
 
         def load_x(c, pool, **place):
             raw = pool.tile([P, 4, CHUNK], F32, name="raw%d" % c, align_bytes=ALIGN, **place)
             nc.sync.dma_start(out=raw[:], in_=x_rows[:, :, c * CHUNK : (c + 1) * CHUNK])
             raws[c] = raw
 
-        def quantise_x(c):
+        def round_x(c):
             cut = VECTOR_TOKENS[c]
             side = keep.tile([P, CHUNK, 4], BF16, name="side%d" % c, tag="side%d" % c, align_bytes=ALIGN)
             source = raws[c][:].rearrange("p j (w n) -> p w j n", n=4)
@@ -91,10 +92,13 @@ def tile_moe_rag_glu_sigmoid_kernel(
             if cut > 0:
                 nc.vector.tensor_copy(out=target[:, : cut // 4], in_=source[:, : cut // 4])
             nc.scalar.copy(out=target[:, cut // 4 :], in_=source[:, cut // 4 :])
+            sides[c] = side
+
+        def quantise_x(c):
             nc.vector.quantize_mx(
                 out=x_words[:, c * CHUNK : (c + 1) * CHUNK].bitcast(FP8X4),
                 scales=x_bytes[:, c * CHUNK : (c + 1) * CHUNK],
-                in_=side[:].rearrange("p w j -> p (w j)"),
+                in_=sides[c][:].rearrange("p w j -> p (w j)"),
             )
 
         def load_words(m, e, pool, **place):
@@ -103,14 +107,23 @@ def tile_moe_rag_glu_sigmoid_kernel(
             nc.sync.dma_start(out=words[:].bitcast(I32), in_=source[e])
             loaded[m, e] = words
 
-        def order_words(m, e):
+        def order_words(m, e, copy):
             ordered = keep.tile([P, 2 * H], U8, name="ordered%d%d" % (m, e), align_bytes=ALIGN)
-            nc.vector.tensor_copy(
+            copy(
                 out=ordered[:].bitcast(U16).rearrange("p (g t q) -> p g t q", t=4, q=P),
                 in_=loaded[m, e][:].bitcast(U16).rearrange("p (g q t) -> p g t q", t=4, q=P),
             )
             stationary[m, e] = ordered
 
+        def spread_scales(queue, e, plane, piece):
+            for a in range(4):
+                queue.dma_start(
+                    out=plane[32 * a : 32 * a + 4].rearrange("p (x c) -> p x c", c=piece).bitcast(I32),
+                    in_=ordered_rows[64 * e + 16 * a : 64 * e + 16 * (a + 1), :piece].bitcast(I32),
+                )
+
+        offsets = keep.tile([P, T // 16], U16, name="offsets", align_bytes=ALIGN)
+        nc.sync.dma_start(offsets[:], offs)
         load_x(0, keep, tag="raw0")
         load_x(1, keep, tag="raw1")
         load_words(0, 0, keep, tag="loaded00")
@@ -119,11 +132,7 @@ def tile_moe_rag_glu_sigmoid_kernel(
             out=ordered_rows[:, :PASS].rearrange("p (t q) -> p t q", t=4),
             in_=rows[:].rearrange("p (q t) -> p t q", t=4),
         )
-        for a in range(4):
-            nc.sync.dma_start(
-                out=planes[32 * a : 32 * a + 4].rearrange("p (x c) -> p x c", c=PIECE).bitcast(I32),
-                in_=ordered_rows[32 * a : 32 * (a + 1)].bitcast(I32),
-            )
+        spread_scales(nc.sync, 0, first_planes[:], PIECE)
         load_x(2, held, offset=0)
         load_words(1, 0, held, offset=RAW_BYTES)
 
@@ -137,20 +146,25 @@ def tile_moe_rag_glu_sigmoid_kernel(
             nc.vector.tensor_copy(scale[:], x_bytes[:, : reach(b)].indirect(listed))
             slot_words[b], slot_bytes[b] = words, scale
 
-        order = [0, 1, 2, 5, 6, 7, 3, 4]
+        order = [0, 1, 2, 3, 5, 6, 7, 4]
+        round_x(0)
         quantise_x(0)
         load_x(3, keep, tag="raw0")
+        round_x(1)
         quantise_x(1)
+        order_words(0, 0, nc.scalar.copy)
         load_words(0, 1, keep, tag="raw1")
-        order_words(0, 0)
-        load_words(1, 1, keep, tag="loaded00")
-        gather(order[0])
-        order_words(1, 0)
-        gate_sb = keep.tile([P, T], F32, name="gate_sb", tag="side1", align_bytes=ALIGN)
-        nc.sync.dma_start(out=gate_sb[:], in_=gate)
-        w2_sb = keep.tile([P, E * GROUPS, 2 * N], U8, name="w2_sb", tag="side0", align_bytes=ALIGN)
+        load_words(1, 1, keep, tag="side0")
+        w2_sb = keep.tile([P, E * GROUPS, 2 * N], U8, name="w2_sb", tag="side1", align_bytes=ALIGN)
         nc.sync.dma_start(out=w2_sb[:].bitcast(I32), in_=w2_words.rearrange("e s p n -> p (e s) n").bitcast(I32))
+        gate_sb = keep.tile([P, T], F32, name="gate_sb", tag="loaded00", align_bytes=ALIGN)
+        nc.sync.dma_start(out=gate_sb[:], in_=gate)
+        gather(order[0])
+        round_x(2)
+        order_words(1, 0, nc.vector.tensor_copy)
         quantise_x(2)
+        spread_scales(nc.sync, 1, late_planes[:], PASS)
+        planes = ((first_planes[:], PIECE), (late_planes[:], PASS))
         gather(order[1])
         gather(order[2])
 
@@ -165,11 +179,11 @@ def tile_moe_rag_glu_sigmoid_kernel(
                 bank = psum.tile([P, 4, P], F32, name=tag, bufs=depth)
                 for t in range(4):
                     at = PASS * g + P * t
-                    column = (4 * g + 2 * e + m) * PIECE + P * t
+                    column = (2 * g + m) * planes[e][1] + P * t
                     nc.tensor.matmul_mx(
                         out=bank[:, t, :],
                         lhsT=stationary[m, e][:, 2 * at : 2 * (at + P)].bitcast(FP4X4),
-                        lhsT_scale=planes[:, column : column + P],
+                        lhsT_scale=planes[e][0][:, column : column + P],
                         rhs=slot_words[b][:].bitcast(FP8X4),
                         rhs_scale=slot_bytes[b][:],
                         start=True,
@@ -207,7 +221,7 @@ def tile_moe_rag_glu_sigmoid_kernel(
                 nc.tensor.matmul_mx(
                     out=y[:],
                     lhsT=w2_sb[:, at, :].bitcast(FP4X4),
-                    lhsT_scale=planes[:, 2 * at * PIECE + PASS : (2 * at + 1) * PIECE],
+                    lhsT_scale=first_planes[:, at * PIECE + PASS : (at + 1) * PIECE],
                     rhs=codes[:, g, :].bitcast(FP8X4),
                     rhs_scale=scale[:, g, :],
                     start=(g == 0),
@@ -215,17 +229,28 @@ def tile_moe_rag_glu_sigmoid_kernel(
                 )
             sums[i] = y
 
-        weighed = {}
+        results = {}
+        early = min(first_slot(b) for b in order[EARLY_STEPS:])
 
-        def weigh(i):
-            b = order[i]
-            weighed[i] = work.tile([P, P], F32, name="weighed", bufs=BLOCKS, align_bytes=ALIGN)
-            nc.vector.tensor_tensor(weighed[i][:], sums[i][:], gate_sb[:, b * P : (b + 1) * P], MULT)
+        def evacuate(i):
+            results[i] = work.tile([P, P], F32, name="result", bufs=BLOCKS, align_bytes=ALIGN)
+            if i in SCALAR_SCATTERS:
+                b = order[i]
+                nc.vector.tensor_tensor(results[i][:], sums[i][:], gate_sb[:, b * P : (b + 1) * P], MULT)
+            else:
+                nc.scalar.copy(out=results[i][:], in_=sums[i][:])
 
         def scatter(i):
             b = order[i]
-            listed = offsets[:, b * LIST_COLUMNS : (b + 1) * LIST_COLUMNS]
-            nc.scalar.activation(outT[:].indirect(listed), weighed[i][:], COPY)
+            window = outT[:].indirect(offsets[:, b * LIST_COLUMNS : (b + 1) * LIST_COLUMNS])
+            if i in SCALAR_SCATTERS:
+                nc.scalar.activation(window, results[i][:], COPY)
+            else:
+                nc.vector.tensor_tensor(window, results[i][:], gate_sb[:, b * P : (b + 1) * P], MULT)
+            if i == EARLY_STEPS - 1:
+                finished = keep.tile([P, early], F32, name="finished", align_bytes=ALIGN)
+                nc.scalar.copy(out=finished[:], in_=outT[:, :early])
+                nc.sync.dma_start(out=out[:, :early], in_=finished[:])
 
         last = BLOCKS - 1
         for i in range(BLOCKS):
@@ -233,23 +258,24 @@ def tile_moe_rag_glu_sigmoid_kernel(
             if i >= 1:
                 quantise_h(i - 1, slice(0, GROUPS))
                 second_layer(i - 1)
-            if i == 0:
-                order_words(0, 1)
-            if i == 1:
-                order_words(1, 1)
             first_layer(i, 1)
+            if i == 0:
+                round_x(3)
+            if i in (2, 3):
+                order_words(i - 2, 1, nc.scalar.copy)
             if i >= SCATTER_LAG:
                 scatter(i - SCATTER_LAG)
             if i == 1:
                 quantise_x(3)
-            if i + GATHER_LEAD < BLOCKS:
+                gather(order[3])
+            if 1 <= i < BLOCKS - GATHER_LEAD:
                 gather(order[i + GATHER_LEAD])
             if i >= 1:
-                weigh(i - 1)
+                evacuate(i - 1)
         quantise_h(last, slice(0, 1))
         quantise_h(last, slice(1, 2))
         second_layer(last)
-        weigh(last)
+        evacuate(last)
         for i in range(BLOCKS - SCATTER_LAG, BLOCKS):
             scatter(i)
-        nc.sync.dma_start(out=out, in_=outT[:])
+        nc.sync.dma_start(out=out[:, early:], in_=outT[:, early:])

@@ -33,7 +33,7 @@ GATED_BUFFERS = 8
 GATHER_LEAD = 3
 SCATTER_LAG = 2
 EARLY_STEPS = 6
-SCALAR_SCATTERS = (1, 3, 5)
+SCALAR_SCATTERS = (1, 2, 3, 4, 5)
 
 
 def expert(b):
@@ -58,7 +58,7 @@ def tile_moe_rag_glu_sigmoid_kernel(
         held = ctx.enter_context(tc.tile_pool(name="held", bufs=1))
         psum = ctx.enter_context(tc.psum_pool(name="psum", bufs=1))
 
-        rows = held.tile([P, PASS], U8, name="rows", offset=RAW_BYTES - ALIGN, align_bytes=ALIGN)
+        rows = held.tile([P, PASS], U8, name="rows", offset=RAW_BYTES - 2 * ALIGN, align_bytes=ALIGN)
         for m, scales in enumerate((w1_scales, w3_scales)):
             halves = scales.rearrange("e s q (g c) -> (e s q g) c", g=GROUPS).bitcast(I32)
             nc.sync.dma_start(out=rows[m:P:2].bitcast(I32), in_=halves)
@@ -122,11 +122,12 @@ def tile_moe_rag_glu_sigmoid_kernel(
                     in_=ordered_rows[64 * e + 16 * a : 64 * e + 16 * (a + 1), :piece].bitcast(I32),
                 )
 
+        load_words(0, 0, keep, tag="loaded00")
+        load_words(1, 0, keep, tag="loaded10")
         offsets = keep.tile([P, T // 16], U16, name="offsets", align_bytes=ALIGN)
         nc.sync.dma_start(offsets[:], offs)
         load_x(0, keep, tag="raw0")
         load_x(1, keep, tag="raw1")
-        load_words(0, 0, keep, tag="loaded00")
 
         nc.vector.tensor_copy(
             out=ordered_rows[:, :PASS].rearrange("p (t q) -> p t q", t=4),
@@ -134,7 +135,8 @@ def tile_moe_rag_glu_sigmoid_kernel(
         )
         spread_scales(nc.sync, 0, first_planes[:], PIECE)
         load_x(2, held, offset=0)
-        load_words(1, 0, held, offset=RAW_BYTES)
+        order_words(0, 0, nc.scalar.copy)
+        order_words(1, 0, nc.vector.tensor_copy)
 
         slot_words, slot_bytes = {}, {}
 
@@ -152,24 +154,22 @@ def tile_moe_rag_glu_sigmoid_kernel(
         load_x(3, keep, tag="raw0")
         round_x(1)
         quantise_x(1)
-        order_words(0, 0, nc.scalar.copy)
         load_words(0, 1, keep, tag="raw1")
         load_words(1, 1, keep, tag="side0")
         w2_sb = keep.tile([P, E * GROUPS, 2 * N], U8, name="w2_sb", tag="side1", align_bytes=ALIGN)
         nc.sync.dma_start(out=w2_sb[:].bitcast(I32), in_=w2_words.rearrange("e s p n -> p (e s) n").bitcast(I32))
-        gate_sb = keep.tile([P, T], F32, name="gate_sb", tag="loaded00", align_bytes=ALIGN)
-        nc.sync.dma_start(out=gate_sb[:], in_=gate)
         gather(order[0])
         round_x(2)
-        order_words(1, 0, nc.vector.tensor_copy)
         quantise_x(2)
+        gate_sb = keep.tile([P, T], F32, name="gate_sb", tag="side2", align_bytes=ALIGN)
+        nc.sync.dma_start(out=gate_sb[:], in_=gate)
         spread_scales(nc.sync, 1, late_planes[:], PASS)
         planes = ((first_planes[:], PIECE), (late_planes[:], PASS))
         gather(order[1])
         gather(order[2])
 
         outT = keep.tile([P, T], F32, name="outT", align_bytes=ALIGN)
-        hidden, sums = {}, {}
+        hidden, sums, factors = {}, {}, {}
 
         def first_layer(i, g):
             b = order[i]
@@ -190,14 +190,18 @@ def tile_moe_rag_glu_sigmoid_kernel(
                         stop=True,
                     )
                 banks.append(bank[:].rearrange("p t s -> p s t"))
-            if g == 0:
-                hidden[i] = work.tile([P, GROUPS, P, 4], BF16, name="hidden", align_bytes=ALIGN)
             if i == 0:
                 gated = held.tile([P, P, 4], F32, name="gated%d" % g, offset=g * PASS * 4, align_bytes=ALIGN)
             else:
                 gated = work.tile([P, P, 4], F32, name="gated", bufs=GATED_BUFFERS, align_bytes=ALIGN)
             nc.scalar.activation(gated[:], banks[0], SIGMOID)
-            nc.vector.tensor_tensor(hidden[i][:, g], banks[1], gated[:], MULT)
+            factors[i, g] = banks[1], gated
+
+        def product(i, g):
+            if g == 0:
+                hidden[i] = work.tile([P, GROUPS, P, 4], BF16, name="hidden", align_bytes=ALIGN)
+            bank, gated = factors[i, g]
+            nc.vector.tensor_tensor(hidden[i][:, g], bank, gated[:], MULT)
 
         quantised = {}
 
@@ -253,16 +257,23 @@ def tile_moe_rag_glu_sigmoid_kernel(
                 nc.sync.dma_start(out=out[:, :early], in_=finished[:])
 
         last = BLOCKS - 1
+        first_layer(0, 0)
+        first_layer(0, 1)
         for i in range(BLOCKS):
-            first_layer(i, 0)
+            if i < last:
+                first_layer(i + 1, 0)
+            product(i, 0)
             if i >= 1:
                 quantise_h(i - 1, slice(0, GROUPS))
+            if i < last:
+                first_layer(i + 1, 1)
+            product(i, 1)
+            if i >= 1:
                 second_layer(i - 1)
-            first_layer(i, 1)
             if i == 0:
                 round_x(3)
-            if i in (2, 3):
-                order_words(i - 2, 1, nc.scalar.copy)
+            if i in (1, 2):
+                order_words(i - 1, 1, nc.scalar.copy)
             if i >= SCATTER_LAG:
                 scatter(i - SCATTER_LAG)
             if i == 1:

@@ -30,8 +30,8 @@ PIECE = PASS + N
 VECTOR_TOKENS = (160, 160, 128, 0)
 A_BANKS, B_BANKS, Y_BANKS = 2, 4, 2
 GATED_BUFFERS = 8
-GATHER_LEAD = 3
-SCATTER_LAG = 2
+GATHER_LEAD = 2
+HELD_STEPS = 3
 EARLY_STEPS = 6
 SCALAR_SCATTERS = (1, 2, 3, 4, 5)
 
@@ -113,7 +113,16 @@ def tile_moe_rag_glu_sigmoid_kernel(
                 out=ordered[:].bitcast(U16).rearrange("p (g t q) -> p g t q", t=4, q=P),
                 in_=loaded[m, e][:].bitcast(U16).rearrange("p (g q t) -> p g t q", t=4, q=P),
             )
-            stationary[m, e] = ordered
+            for g in range(GROUPS):
+                stationary[m, e, g] = ordered[:, 2 * PASS * g : 2 * PASS * (g + 1)]
+
+        def order_half(m, e, g, copy, pool, **place):
+            ordered = pool.tile([P, 2 * PASS], U8, name="ordered%d%d%d" % (m, e, g), align_bytes=ALIGN, **place)
+            copy(
+                out=ordered[:].bitcast(U16).rearrange("p (t q) -> p t q", t=4),
+                in_=loaded[m, e][:, 2 * PASS * g : 2 * PASS * (g + 1)].bitcast(U16).rearrange("p (q t) -> p t q", t=4),
+            )
+            stationary[m, e, g] = ordered[:]
 
         def spread_scales(queue, e, plane, piece):
             for a in range(4):
@@ -166,7 +175,6 @@ def tile_moe_rag_glu_sigmoid_kernel(
         spread_scales(nc.sync, 1, late_planes[:], PASS)
         planes = ((first_planes[:], PIECE), (late_planes[:], PASS))
         gather(order[1])
-        gather(order[2])
 
         outT = keep.tile([P, T], F32, name="outT", align_bytes=ALIGN)
         hidden, sums, factors = {}, {}, {}
@@ -178,11 +186,10 @@ def tile_moe_rag_glu_sigmoid_kernel(
             for m, (tag, depth) in enumerate((("a", A_BANKS), ("b", B_BANKS))):
                 bank = psum.tile([P, 4, P], F32, name=tag, bufs=depth)
                 for t in range(4):
-                    at = PASS * g + P * t
                     column = (2 * g + m) * planes[e][1] + P * t
                     nc.tensor.matmul_mx(
                         out=bank[:, t, :],
-                        lhsT=stationary[m, e][:, 2 * at : 2 * (at + P)].bitcast(FP4X4),
+                        lhsT=stationary[m, e, g][:, 2 * P * t : 2 * P * (t + 1)].bitcast(FP4X4),
                         lhsT_scale=planes[e][0][:, column : column + P],
                         rhs=slot_words[b][:].bitcast(FP8X4),
                         rhs_scale=slot_bytes[b][:],
@@ -198,7 +205,11 @@ def tile_moe_rag_glu_sigmoid_kernel(
             factors[i, g] = banks[1], gated
 
         def product(i, g):
-            if g == 0:
+            if g == 0 and i < HELD_STEPS:
+                hidden[i] = held.tile(
+                    [P, GROUPS, P, 4], BF16, name="hidden%d" % i, offset=RAW_BYTES + 2 * H * i, align_bytes=ALIGN
+                )
+            elif g == 0:
                 hidden[i] = work.tile([P, GROUPS, P, 4], BF16, name="hidden", align_bytes=ALIGN)
             bank, gated = factors[i, g]
             nc.vector.tensor_tensor(hidden[i][:, g], bank, gated[:], MULT)
@@ -263,30 +274,32 @@ def tile_moe_rag_glu_sigmoid_kernel(
             if i < last:
                 first_layer(i + 1, 0)
             product(i, 0)
-            if i >= 1:
-                quantise_h(i - 1, slice(0, GROUPS))
+            if i == 0:
+                gather(order[GATHER_LEAD])
             if i < last:
                 first_layer(i + 1, 1)
             product(i, 1)
-            if i >= 1:
-                second_layer(i - 1)
             if i == 0:
                 round_x(3)
-            if i in (1, 2):
-                order_words(i - 1, 1, nc.scalar.copy)
-            if i >= SCATTER_LAG:
-                scatter(i - SCATTER_LAG)
             if i == 1:
                 quantise_x(3)
-                gather(order[3])
+                order_half(0, 1, 1, nc.scalar.copy, keep)
             if 1 <= i < BLOCKS - GATHER_LEAD:
                 gather(order[i + GATHER_LEAD])
+            if i == last:
+                break
             if i >= 1:
                 evacuate(i - 1)
+                scatter(i - 1)
+            quantise_h(i, slice(0, GROUPS))
+            second_layer(i)
+            if i < HELD_STEPS:
+                m, g = ((0, 0), (1, 0), (1, 1))[i]
+                order_half(m, 1, g, nc.gpsimd.tensor_copy, held, offset=RAW_BYTES + 2 * H * i)
         quantise_h(last, slice(0, 1))
         quantise_h(last, slice(1, 2))
         second_layer(last)
-        evacuate(last)
-        for i in range(BLOCKS - SCATTER_LAG, BLOCKS):
+        for i in (last - 1, last):
+            evacuate(i)
             scatter(i)
         nc.sync.dma_start(out=out[:, early:], in_=outT[:, early:])

@@ -31,6 +31,7 @@ VECTOR_TOKENS = (160, 160, 128, 0)
 A_BANKS, B_BANKS, Y_BANKS = 2, 4, 2
 GATED_BUFFERS = 8
 GATHER_LEAD = 2
+FIRST_GATES = 2 * P
 HELD_STEPS = 3
 EARLY_STEPS = 6
 SCALAR_SCATTERS = (1, 2, 3, 4, 5)
@@ -58,7 +59,7 @@ def tile_moe_rag_glu_sigmoid_kernel(
         held = ctx.enter_context(tc.tile_pool(name="held", bufs=1))
         psum = ctx.enter_context(tc.psum_pool(name="psum", bufs=1))
 
-        rows = held.tile([P, PASS], U8, name="rows", offset=RAW_BYTES - 2 * ALIGN, align_bytes=ALIGN)
+        rows = held.tile([P, PASS], U8, name="rows", offset=RAW_BYTES - ALIGN, align_bytes=ALIGN)
         for m, scales in enumerate((w1_scales, w3_scales)):
             halves = scales.rearrange("e s q (g c) -> (e s q g) c", g=GROUPS).bitcast(I32)
             nc.sync.dma_start(out=rows[m:P:2].bitcast(I32), in_=halves)
@@ -107,15 +108,6 @@ def tile_moe_rag_glu_sigmoid_kernel(
             nc.sync.dma_start(out=words[:].bitcast(I32), in_=source[e])
             loaded[m, e] = words
 
-        def order_words(m, e, copy):
-            ordered = keep.tile([P, 2 * H], U8, name="ordered%d%d" % (m, e), align_bytes=ALIGN)
-            copy(
-                out=ordered[:].bitcast(U16).rearrange("p (g t q) -> p g t q", t=4, q=P),
-                in_=loaded[m, e][:].bitcast(U16).rearrange("p (g q t) -> p g t q", t=4, q=P),
-            )
-            for g in range(GROUPS):
-                stationary[m, e, g] = ordered[:, 2 * PASS * g : 2 * PASS * (g + 1)]
-
         def order_half(m, e, g, copy, pool, **place):
             ordered = pool.tile([P, 2 * PASS], U8, name="ordered%d%d%d" % (m, e, g), align_bytes=ALIGN, **place)
             copy(
@@ -125,18 +117,17 @@ def tile_moe_rag_glu_sigmoid_kernel(
             stationary[m, e, g] = ordered[:]
 
         def spread_scales(queue, e, plane, piece):
-            for a in range(4):
+            for a in (0, 2, 1, 3):
                 queue.dma_start(
                     out=plane[32 * a : 32 * a + 4].rearrange("p (x c) -> p x c", c=piece).bitcast(I32),
                     in_=ordered_rows[64 * e + 16 * a : 64 * e + 16 * (a + 1), :piece].bitcast(I32),
                 )
 
-        load_words(0, 0, keep, tag="loaded00")
-        load_words(1, 0, keep, tag="loaded10")
         offsets = keep.tile([P, T // 16], U16, name="offsets", align_bytes=ALIGN)
         nc.sync.dma_start(offsets[:], offs)
         load_x(0, keep, tag="raw0")
         load_x(1, keep, tag="raw1")
+        load_words(0, 0, keep, tag="loaded00")
 
         nc.vector.tensor_copy(
             out=ordered_rows[:, :PASS].rearrange("p (t q) -> p t q", t=4),
@@ -144,8 +135,7 @@ def tile_moe_rag_glu_sigmoid_kernel(
         )
         spread_scales(nc.sync, 0, first_planes[:], PIECE)
         load_x(2, held, offset=0)
-        order_words(0, 0, nc.scalar.copy)
-        order_words(1, 0, nc.vector.tensor_copy)
+        load_words(1, 0, held, offset=RAW_BYTES)
 
         slot_words, slot_bytes = {}, {}
 
@@ -163,16 +153,27 @@ def tile_moe_rag_glu_sigmoid_kernel(
         load_x(3, keep, tag="raw0")
         round_x(1)
         quantise_x(1)
+        order_half(0, 0, 0, nc.scalar.copy, keep)
+        order_half(0, 0, 1, nc.scalar.copy, keep)
         load_words(0, 1, keep, tag="raw1")
-        load_words(1, 1, keep, tag="side0")
-        w2_sb = keep.tile([P, E * GROUPS, 2 * N], U8, name="w2_sb", tag="side1", align_bytes=ALIGN)
+        w2_sb = keep.tile([P, E * GROUPS, 2 * N], U8, name="w2_sb", tag="side0", align_bytes=ALIGN)
         nc.sync.dma_start(out=w2_sb[:].bitcast(I32), in_=w2_words.rearrange("e s p n -> p (e s) n").bitcast(I32))
+        first_gates = keep.tile([P, FIRST_GATES], F32, name="first_gates", tag="side1", align_bytes=ALIGN)
+        nc.sync.dma_start(out=first_gates[:], in_=gate[:, :FIRST_GATES])
+        load_words(1, 1, keep, tag="loaded11")
         gather(order[0])
         round_x(2)
+        order_half(1, 0, 0, nc.vector.tensor_copy, keep)
         quantise_x(2)
-        gate_sb = keep.tile([P, T], F32, name="gate_sb", tag="side2", align_bytes=ALIGN)
-        nc.sync.dma_start(out=gate_sb[:], in_=gate)
         spread_scales(nc.sync, 1, late_planes[:], PASS)
+        late_gates = keep.tile([P, T - FIRST_GATES], F32, name="late_gates", tag="side2", align_bytes=ALIGN)
+        nc.sync.dma_start(out=late_gates[:], in_=gate[:, FIRST_GATES:])
+
+        def gates(b):
+            if b * P < FIRST_GATES:
+                return first_gates[:, b * P : (b + 1) * P]
+            return late_gates[:, b * P - FIRST_GATES : (b + 1) * P - FIRST_GATES]
+
         planes = ((first_planes[:], PIECE), (late_planes[:], PASS))
         gather(order[1])
 
@@ -207,7 +208,7 @@ def tile_moe_rag_glu_sigmoid_kernel(
         def product(i, g):
             if g == 0 and i < HELD_STEPS:
                 hidden[i] = held.tile(
-                    [P, GROUPS, P, 4], BF16, name="hidden%d" % i, offset=RAW_BYTES + 2 * H * i, align_bytes=ALIGN
+                    [P, GROUPS, P, 4], BF16, name="hidden%d" % i, offset=RAW_BYTES + 2 * H * (i + 1), align_bytes=ALIGN
                 )
             elif g == 0:
                 hidden[i] = work.tile([P, GROUPS, P, 4], BF16, name="hidden", align_bytes=ALIGN)
@@ -251,7 +252,7 @@ def tile_moe_rag_glu_sigmoid_kernel(
             results[i] = work.tile([P, P], F32, name="result", bufs=BLOCKS, align_bytes=ALIGN)
             if i in SCALAR_SCATTERS:
                 b = order[i]
-                nc.vector.tensor_tensor(results[i][:], sums[i][:], gate_sb[:, b * P : (b + 1) * P], MULT)
+                nc.vector.tensor_tensor(results[i][:], sums[i][:], gates(b), MULT)
             else:
                 nc.scalar.copy(out=results[i][:], in_=sums[i][:])
 
@@ -261,7 +262,7 @@ def tile_moe_rag_glu_sigmoid_kernel(
             if i in SCALAR_SCATTERS:
                 nc.scalar.activation(window, results[i][:], COPY)
             else:
-                nc.vector.tensor_tensor(window, results[i][:], gate_sb[:, b * P : (b + 1) * P], MULT)
+                nc.vector.tensor_tensor(window, results[i][:], gates(b), MULT)
             if i == EARLY_STEPS - 1:
                 finished = keep.tile([P, early], F32, name="finished", align_bytes=ALIGN)
                 nc.scalar.copy(out=finished[:], in_=outT[:, :early])
@@ -269,8 +270,11 @@ def tile_moe_rag_glu_sigmoid_kernel(
 
         last = BLOCKS - 1
         first_layer(0, 0)
+        order_half(1, 0, 1, nc.scalar.copy, keep)
         first_layer(0, 1)
         for i in range(BLOCKS):
+            if i >= 1 and i - 1 not in SCALAR_SCATTERS:
+                evacuate(i - 1)
             if i < last:
                 first_layer(i + 1, 0)
             product(i, 0)
@@ -288,18 +292,19 @@ def tile_moe_rag_glu_sigmoid_kernel(
                 gather(order[i + GATHER_LEAD])
             if i == last:
                 break
-            if i >= 1:
+            if i - 1 in SCALAR_SCATTERS:
                 evacuate(i - 1)
+            if i >= 1:
                 scatter(i - 1)
             quantise_h(i, slice(0, GROUPS))
             second_layer(i)
             if i < HELD_STEPS:
                 m, g = ((0, 0), (1, 0), (1, 1))[i]
-                order_half(m, 1, g, nc.gpsimd.tensor_copy, held, offset=RAW_BYTES + 2 * H * i)
+                order_half(m, 1, g, nc.gpsimd.tensor_copy, held, offset=RAW_BYTES + 2 * H * (i + 1))
         quantise_h(last, slice(0, 1))
         quantise_h(last, slice(1, 2))
         second_layer(last)
-        for i in (last - 1, last):
-            evacuate(i)
-            scatter(i)
+        scatter(last - 1)
+        evacuate(last)
+        scatter(last)
         nc.sync.dma_start(out=out[:, early:], in_=outT[:, early:])

@@ -27,7 +27,7 @@ ALIGN = 256
 CHUNK = 256
 RAW_BYTES = 4 * CHUNK * 4
 PIECE = PASS + N
-VECTOR_TOKENS = (160, 160, 128, 0)
+VECTOR_TOKENS = (160, 160, 128, 128)
 A_BANKS, B_BANKS, Y_BANKS = 2, 4, 2
 GATED_BUFFERS = 8
 GATHER_LEAD = 2
@@ -246,7 +246,9 @@ def tile_moe_rag_glu_sigmoid_kernel(
             sums[i] = y
 
         results = {}
-        early = min(first_slot(b) for b in order[EARLY_STEPS:])
+
+        def final_below(i):
+            return min([T] + [first_slot(b) for b in order[i + 1 :]])
 
         def evacuate(i):
             results[i] = work.tile([P, P], F32, name="result", bufs=BLOCKS, align_bytes=ALIGN)
@@ -263,10 +265,16 @@ def tile_moe_rag_glu_sigmoid_kernel(
                 nc.scalar.activation(window, results[i][:], COPY)
             else:
                 nc.vector.tensor_tensor(window, results[i][:], gates(b), MULT)
-            if i == EARLY_STEPS - 1:
-                finished = keep.tile([P, early], F32, name="finished", align_bytes=ALIGN)
-                nc.scalar.copy(out=finished[:], in_=outT[:, :early])
-                nc.sync.dma_start(out=out[:, :early], in_=finished[:])
+            if i >= EARLY_STEPS - 1:
+                start = final_below(i - 1) if i >= EARLY_STEPS else 0
+                columns = slice(start, final_below(i))
+                if i == BLOCKS - 1:
+                    nc.sync.dma_start(out=out[:, columns], in_=outT[:, columns])
+                else:
+                    copy = nc.scalar.copy if i in SCALAR_SCATTERS else nc.vector.tensor_copy
+                    finished = keep.tile([P, columns.stop - start], F32, name="finished%d" % i, align_bytes=ALIGN)
+                    copy(out=finished[:], in_=outT[:, columns])
+                    nc.sync.dma_start(out=out[:, columns], in_=finished[:])
 
         last = BLOCKS - 1
         first_layer(0, 0)
@@ -279,14 +287,14 @@ def tile_moe_rag_glu_sigmoid_kernel(
                 first_layer(i + 1, 0)
             product(i, 0)
             if i == 0:
+                round_x(3)
                 gather(order[GATHER_LEAD])
             if i < last:
                 first_layer(i + 1, 1)
             product(i, 1)
             if i == 0:
-                round_x(3)
-            if i == 1:
                 quantise_x(3)
+            if i == 1:
                 order_half(0, 1, 1, nc.scalar.copy, keep)
             if 1 <= i < BLOCKS - GATHER_LEAD:
                 gather(order[i + GATHER_LEAD])
@@ -307,4 +315,3 @@ def tile_moe_rag_glu_sigmoid_kernel(
         scatter(last - 1)
         evacuate(last)
         scatter(last)
-        nc.sync.dma_start(out=out[:, early:], in_=outT[:, early:])

@@ -34,7 +34,7 @@ GATHER_LEAD = 2
 FIRST_GATES = 2 * P
 HELD_STEPS = 3
 EARLY_STEPS = 6
-SCALAR_SCATTERS = (1, 2, 3, 4, 5)
+SCALAR_SCATTERS = (0, 1, 2, 3, 4, 5)
 
 
 def expert(b):

from contextlib import ExitStack

import concourse.mybir as mybir

K, T, E, H, N = 512, 1024, 2, 1024, 128
COUNTS = (640, 384)
FLOPS = 2 * T * (2 * K * H + H * N)

P = 128
F32 = mybir.dt.float32
BF16 = mybir.dt.bfloat16
I32 = mybir.dt.int32
U32 = mybir.dt.uint32
U16 = mybir.dt.uint16
U8 = mybir.dt.uint8
FP8X4 = mybir.dt.float8_e4m3fn_x4
FP4X4 = mybir.dt.float4_e2m1fn_x4
MULT = mybir.AluOpType.mult
SIGMOID = mybir.ActivationFunctionType.Sigmoid
COPY = mybir.ActivationFunctionType.Copy

PASS = 4 * P
GROUPS = H // PASS
BLOCKS = T // P
LIST_COLUMNS = P // 16
ALIGN = 256
CHUNK = 256
RAW_BYTES = 4 * CHUNK * 4
PIECE = PASS + N
VECTOR_TOKENS = (160, 160, 128, 128)
A_BANKS, B_BANKS, Y_BANKS = 2, 4, 2
GATED_BUFFERS = 8
GATHER_LEAD = 2
FIRST_GATES = 2 * P
HELD_STEPS = 3
EARLY_STEPS = 6
SCALAR_SCATTERS = (0, 1, 2, 3, 4, 5)


def expert(b):
    return 0 if b * P < COUNTS[0] else 1


def first_slot(b):
    return b * P - sum(COUNTS[: expert(b)])


def reach(b):
    return first_slot(b) + P + T - COUNTS[expert(b)]


def tile_moe_rag_glu_sigmoid_kernel(
    tc, xT, w1_words, w1_scales, w3_words, w3_scales, w2_words, w2_scales, gate, offs, out
):
    nc = tc.nc
    with ExitStack() as ctx:
        keep = ctx.enter_context(tc.tile_pool(name="keep", bufs=1))
        work = ctx.enter_context(tc.tile_pool(name="work", bufs=3))
        held = ctx.enter_context(tc.tile_pool(name="held", bufs=1))
        psum = ctx.enter_context(tc.psum_pool(name="psum", bufs=1))

        rows = held.tile([P, PASS], U8, name="rows", offset=RAW_BYTES - ALIGN, align_bytes=ALIGN)
        for m, scales in enumerate((w1_scales, w3_scales)):
            halves = scales.rearrange("e s q (g c) -> (e s q g) c", g=GROUPS).bitcast(I32)
            nc.sync.dma_start(out=rows[m:P:2].bitcast(I32), in_=halves)
        ordered_rows = keep.tile([P, PIECE], U8, name="ordered_rows", align_bytes=ALIGN)
        nc.sync.dma_start(
            out=ordered_rows[: P // 2, PASS:].bitcast(I32), in_=w2_scales.rearrange("e s q n -> q (e s) n").bitcast(I32)
        )
        warm = keep.tile([P, 1], F32, name="warm")
        nc.vector.memset(warm[:], 0.0)
        nc.scalar.activation(warm[:], warm[:], SIGMOID)
        first_planes = keep.tile([P, 4 * PIECE], U8, name="first_planes", align_bytes=ALIGN)
        nc.vector.memset(first_planes[:].bitcast(I32), 0)
        x_bytes = keep.tile([P, T], U8, name="x_bytes", align_bytes=ALIGN)
        nc.vector.memset(x_bytes[:].bitcast(I32), 0)
        late_planes = keep.tile([P, 4 * PASS], U8, name="late_planes", align_bytes=ALIGN)
        nc.vector.memset(late_planes[:].bitcast(I32), 0)
        x_words = keep.tile([P, T], U32, name="x_words", align_bytes=ALIGN)
        x_rows = xT.rearrange("(p j) w -> p j w", j=4)
        raws, sides, loaded, stationary = {}, {}, {}, {}

        def load_x(c, pool, **place):
            raw = pool.tile([P, 4, CHUNK], F32, name="raw%d" % c, align_bytes=ALIGN, **place)
            nc.sync.dma_start(out=raw[:], in_=x_rows[:, :, c * CHUNK : (c + 1) * CHUNK])
            raws[c] = raw

        def round_x(c):
            cut = VECTOR_TOKENS[c]
            side = keep.tile([P, CHUNK, 4], BF16, name="side%d" % c, tag="side%d" % c, align_bytes=ALIGN)
            source = raws[c][:].rearrange("p j (w n) -> p w j n", n=4)
            target = side[:].rearrange("p (w n) j -> p w j n", n=4)
            if cut > 0:
                nc.vector.tensor_copy(out=target[:, : cut // 4], in_=source[:, : cut // 4])
            nc.scalar.copy(out=target[:, cut // 4 :], in_=source[:, cut // 4 :])
            sides[c] = side

        def quantise_x(c):
            nc.vector.quantize_mx(
                out=x_words[:, c * CHUNK : (c + 1) * CHUNK].bitcast(FP8X4),
                scales=x_bytes[:, c * CHUNK : (c + 1) * CHUNK],
                in_=sides[c][:].rearrange("p w j -> p (w j)"),
            )

        def load_words(m, e, pool, **place):
            words = pool.tile([P, 2 * H], U8, name="loaded%d%d" % (m, e), align_bytes=ALIGN, **place)
            source = (w1_words, w3_words)[m].rearrange("e s p i -> (e s) p i").bitcast(I32)
            nc.sync.dma_start(out=words[:].bitcast(I32), in_=source[e])
            loaded[m, e] = words

        def order_half(m, e, g, copy, pool, **place):
            ordered = pool.tile([P, 2 * PASS], U8, name="ordered%d%d%d" % (m, e, g), align_bytes=ALIGN, **place)
            copy(
                out=ordered[:].bitcast(U16).rearrange("p (t q) -> p t q", t=4),
                in_=loaded[m, e][:, 2 * PASS * g : 2 * PASS * (g + 1)].bitcast(U16).rearrange("p (q t) -> p t q", t=4),
            )
            stationary[m, e, g] = ordered[:]

        def spread_scales(queue, e, plane, piece):
            for a in (0, 2, 1, 3):
                queue.dma_start(
                    out=plane[32 * a : 32 * a + 4].rearrange("p (x c) -> p x c", c=piece).bitcast(I32),
                    in_=ordered_rows[64 * e + 16 * a : 64 * e + 16 * (a + 1), :piece].bitcast(I32),
                )

        offsets = keep.tile([P, T // 16], U16, name="offsets", align_bytes=ALIGN)
        nc.sync.dma_start(offsets[:], offs)
        load_x(0, keep, tag="raw0")
        load_x(1, keep, tag="raw1")
        load_words(0, 0, keep, tag="loaded00")

        nc.vector.tensor_copy(
            out=ordered_rows[:, :PASS].rearrange("p (t q) -> p t q", t=4),
            in_=rows[:].rearrange("p (q t) -> p t q", t=4),
        )
        spread_scales(nc.sync, 0, first_planes[:], PIECE)
        load_x(2, held, offset=0)
        load_words(1, 0, held, offset=RAW_BYTES)

        slot_words, slot_bytes = {}, {}

        def gather(b):
            listed = offsets[:, b * LIST_COLUMNS : (b + 1) * LIST_COLUMNS]
            words = work.tile([P, P], U32, name="slot_words", bufs=GATHER_LEAD + 1, align_bytes=ALIGN)
            nc.vector.tensor_copy(words[:], x_words[:, : reach(b)].indirect(listed))
            scale = work.tile([P, P], U8, name="slot_bytes", bufs=GATHER_LEAD + 1, align_bytes=ALIGN)
            nc.vector.tensor_copy(scale[:], x_bytes[:, : reach(b)].indirect(listed))
            slot_words[b], slot_bytes[b] = words, scale

        order = [0, 1, 2, 3, 5, 6, 7, 4]
        round_x(0)
        quantise_x(0)
        load_x(3, keep, tag="raw0")
        round_x(1)
        quantise_x(1)
        order_half(0, 0, 0, nc.scalar.copy, keep)
        order_half(0, 0, 1, nc.scalar.copy, keep)
        load_words(0, 1, keep, tag="raw1")
        w2_sb = keep.tile([P, E * GROUPS, 2 * N], U8, name="w2_sb", tag="side0", align_bytes=ALIGN)
        nc.sync.dma_start(out=w2_sb[:].bitcast(I32), in_=w2_words.rearrange("e s p n -> p (e s) n").bitcast(I32))
        first_gates = keep.tile([P, FIRST_GATES], F32, name="first_gates", tag="side1", align_bytes=ALIGN)
        nc.sync.dma_start(out=first_gates[:], in_=gate[:, :FIRST_GATES])
        load_words(1, 1, keep, tag="loaded11")
        gather(order[0])
        round_x(2)
        order_half(1, 0, 0, nc.vector.tensor_copy, keep)
        quantise_x(2)
        spread_scales(nc.sync, 1, late_planes[:], PASS)
        late_gates = keep.tile([P, T - FIRST_GATES], F32, name="late_gates", tag="side2", align_bytes=ALIGN)
        nc.sync.dma_start(out=late_gates[:], in_=gate[:, FIRST_GATES:])

        def gates(b):
            if b * P < FIRST_GATES:
                return first_gates[:, b * P : (b + 1) * P]
            return late_gates[:, b * P - FIRST_GATES : (b + 1) * P - FIRST_GATES]

        planes = ((first_planes[:], PIECE), (late_planes[:], PASS))
        gather(order[1])

        outT = keep.tile([P, T], F32, name="outT", align_bytes=ALIGN)
        hidden, sums, factors = {}, {}, {}

        def first_layer(i, g):
            b = order[i]
            e = expert(b)
            banks = []
            for m, (tag, depth) in enumerate((("a", A_BANKS), ("b", B_BANKS))):
                bank = psum.tile([P, 4, P], F32, name=tag, bufs=depth)
                for t in range(4):
                    column = (2 * g + m) * planes[e][1] + P * t
                    nc.tensor.matmul_mx(
                        out=bank[:, t, :],
                        lhsT=stationary[m, e, g][:, 2 * P * t : 2 * P * (t + 1)].bitcast(FP4X4),
                        lhsT_scale=planes[e][0][:, column : column + P],
                        rhs=slot_words[b][:].bitcast(FP8X4),
                        rhs_scale=slot_bytes[b][:],
                        start=True,
                        stop=True,
                    )
                banks.append(bank[:].rearrange("p t s -> p s t"))
            if i == 0:
                gated = held.tile([P, P, 4], F32, name="gated%d" % g, offset=g * PASS * 4, align_bytes=ALIGN)
            else:
                gated = work.tile([P, P, 4], F32, name="gated", bufs=GATED_BUFFERS, align_bytes=ALIGN)
            nc.scalar.activation(gated[:], banks[0], SIGMOID)
            factors[i, g] = banks[1], gated

        def product(i, g):
            if g == 0 and i < HELD_STEPS:
                hidden[i] = held.tile(
                    [P, GROUPS, P, 4], BF16, name="hidden%d" % i, offset=RAW_BYTES + 2 * H * (i + 1), align_bytes=ALIGN
                )
            elif g == 0:
                hidden[i] = work.tile([P, GROUPS, P, 4], BF16, name="hidden", align_bytes=ALIGN)
            bank, gated = factors[i, g]
            nc.vector.tensor_tensor(hidden[i][:, g], bank, gated[:], MULT)

        quantised = {}

        def quantise_h(i, passes):
            if passes.start == 0:
                codes = work.tile([P, GROUPS, P], U32, name="codes", align_bytes=ALIGN)
                scale = work.tile([P, GROUPS, P], U8, name="scale", align_bytes=ALIGN)
                quantised[i] = codes, scale
            codes, scale = quantised[i]
            nc.vector.quantize_mx(
                out=codes[:, passes].rearrange("p g s -> p (g s)").bitcast(FP8X4),
                scales=scale[:, passes].rearrange("p g s -> p (g s)"),
                in_=hidden[i][:, passes].rearrange("p g s t -> p (g s t)"),
            )

        def second_layer(i):
            codes, scale = quantised[i]
            y = psum.tile([P, P], F32, name="y", bufs=Y_BANKS)
            for g in range(GROUPS):
                at = expert(order[i]) * GROUPS + g
                nc.tensor.matmul_mx(
                    out=y[:],
                    lhsT=w2_sb[:, at, :].bitcast(FP4X4),
                    lhsT_scale=first_planes[:, at * PIECE + PASS : (at + 1) * PIECE],
                    rhs=codes[:, g, :].bitcast(FP8X4),
                    rhs_scale=scale[:, g, :],
                    start=(g == 0),
                    stop=(g == GROUPS - 1),
                )
            sums[i] = y

        results = {}

        def final_below(i):
            return min([T] + [first_slot(b) for b in order[i + 1 :]])

        def evacuate(i):
            results[i] = work.tile([P, P], F32, name="result", bufs=BLOCKS, align_bytes=ALIGN)
            if i in SCALAR_SCATTERS:
                b = order[i]
                nc.vector.tensor_tensor(results[i][:], sums[i][:], gates(b), MULT)
            else:
                nc.scalar.copy(out=results[i][:], in_=sums[i][:])

        def scatter(i):
            b = order[i]
            window = outT[:].indirect(offsets[:, b * LIST_COLUMNS : (b + 1) * LIST_COLUMNS])
            if i in SCALAR_SCATTERS:
                nc.scalar.activation(window, results[i][:], COPY)
            else:
                nc.vector.tensor_tensor(window, results[i][:], gates(b), MULT)
            if i >= EARLY_STEPS - 1:
                start = final_below(i - 1) if i >= EARLY_STEPS else 0
                columns = slice(start, final_below(i))
                if i == BLOCKS - 1:
                    nc.sync.dma_start(out=out[:, columns], in_=outT[:, columns])
                else:
                    copy = nc.scalar.copy if i in SCALAR_SCATTERS else nc.vector.tensor_copy
                    finished = keep.tile([P, columns.stop - start], F32, name="finished%d" % i, align_bytes=ALIGN)
                    copy(out=finished[:], in_=outT[:, columns])
                    nc.sync.dma_start(out=out[:, columns], in_=finished[:])

        last = BLOCKS - 1
        first_layer(0, 0)
        order_half(1, 0, 1, nc.scalar.copy, keep)
        first_layer(0, 1)
        for i in range(BLOCKS):
            if i >= 1 and i - 1 not in SCALAR_SCATTERS:
                evacuate(i - 1)
            if i < last:
                first_layer(i + 1, 0)
            product(i, 0)
            if i == 0:
                round_x(3)
                gather(order[GATHER_LEAD])
            if i < last:
                first_layer(i + 1, 1)
            product(i, 1)
            if i == 0:
                quantise_x(3)
            if i == 1:
                order_half(0, 1, 1, nc.scalar.copy, keep)
            if 1 <= i < BLOCKS - GATHER_LEAD:
                gather(order[i + GATHER_LEAD])
            if i == last:
                break
            if i - 1 in SCALAR_SCATTERS:
                evacuate(i - 1)
            if i >= 1:
                scatter(i - 1)
            quantise_h(i, slice(0, GROUPS))
            second_layer(i)
            if i < HELD_STEPS:
                m, g = ((0, 0), (1, 0), (1, 1))[i]
                order_half(m, 1, g, nc.gpsimd.tensor_copy, held, offset=RAW_BYTES + 2 * H * (i + 1))
        quantise_h(last, slice(0, 1))
        quantise_h(last, slice(1, 2))
        second_layer(last)
        scatter(last - 1)
        evacuate(last)
        scatter(last)
